import numpy as np
import ml_dtypes


def mxq(x, axis, fmt="e4m3"):
    dtype, down = {"e4m3": (ml_dtypes.float8_e4m3fn, 7), "e5m2": (ml_dtypes.float8_e5m2, 14)}[fmt]
    v = np.moveaxis(np.asarray(x, np.float32).astype(ml_dtypes.bfloat16).astype(np.float64), axis, -1)
    blocks = v.reshape(v.shape[:-1] + (-1, 32))
    amax = np.abs(blocks).max(-1, keepdims=True)
    byte = np.maximum(np.where(amax > 0, np.frexp(amax)[1] - 1 + 127, 0) - down, 1)
    scale = np.exp2(byte - 127.0)
    codes = (blocks / scale).astype(np.float32).astype(dtype).astype(np.float64)
    return np.moveaxis((codes * scale).reshape(v.shape), -1, axis)


WIDE = False


def mx_kscale(k):
    if not WIDE:
        return np.ones(k)
    levels = np.array([10, -10, 5, -5, 0])
    if k % 512:
        return np.exp2(np.random.permutation(np.resize(levels, k // 32))).repeat(32)
    a = np.empty((k // 512, 16))
    for p in range(k // 512):
        a[p, :8] = np.random.permutation(np.resize(levels, 8))
        for g in range(8):
            far = levels[np.abs(levels - a[p, g]) >= 10]
            a[p, g + 8] = far[np.random.randint(len(far))]
    return np.exp2(a.ravel()).repeat(32)


def f64(x):
    return np.asarray(x).astype(np.float64)


def striped(idx):
    return np.tile(idx.reshape(-1, 16).T, (8, 1)).astype(np.uint16)


def unstriped(offs):
    return offs[:16].T.reshape(-1).astype(np.int64)


E2M1 = np.array([0.0, 0.5, 1.0, 1.5, 2.0, 3.0, 4.0, 6.0, -0.0, -0.5, -1.0, -1.5, -2.0, -3.0, -4.0, -6.0])


def pack_weight(w, fmt):
    k, n = w.shape
    w = f64(np.asarray(w, np.float32).astype(ml_dtypes.bfloat16)).reshape(k // 32, 32, n)
    amax = np.abs(w).max(1)
    if fmt == "e4m3":
        byte = np.frexp(amax)[1] - 1 + 127 - 7
    else:
        mant, ex = np.frexp(amax / 6.0)
        byte = np.where(mant > 0.5, ex, ex - 1) + 127
    byte = np.clip(np.where(amax > 0, byte, 1), 1, 254)
    scaled = (w * np.exp2(127.0 - byte)[:, None, :]).reshape(k, n).astype(np.float32)
    by_word = np.ascontiguousarray(scaled.reshape(k // 512, 128, 4, n).transpose(0, 1, 3, 2))
    if fmt == "e4m3":
        words = by_word.astype(ml_dtypes.float8_e4m3fn).view(np.uint8)
    else:
        c = by_word.astype(ml_dtypes.float4_e2m1fn).view(np.uint8) & 0xF
        words = (c[..., 0::2] | (c[..., 1::2] << 4)).reshape(k // 512, 128, 2 * n)
    return np.ascontiguousarray(words), np.ascontiguousarray(byte.astype(np.uint8).reshape(k // 512, 16, n))


def unpack_weight(words, scales, fmt):
    g, _, n = scales.shape
    words = np.ascontiguousarray(words).reshape(g, 128, n, -1)
    if fmt == "e4m3":
        vals = words.view(ml_dtypes.float8_e4m3fn).astype(np.float64)
    else:
        nib = np.empty((g, 128, n, 4), np.uint8)
        nib[..., 0::2] = words & 0xF
        nib[..., 1::2] = words >> 4
        vals = E2M1[nib]
    vals = vals * np.repeat(np.exp2(scales.astype(np.float64) - 127.0), 8, axis=1)[..., None]
    return vals.transpose(0, 1, 3, 2).reshape(g * 512, n)


def gelu(v):
    return 0.5 * v * (1.0 + np.tanh(np.sqrt(2.0 / np.pi) * (v + 0.044715 * v**3)))


def bf(x):
    return np.asarray(x, np.float32).astype(ml_dtypes.bfloat16)


def planes(Y):
    n, m = Y.shape
    b = f64(bf(Y)).reshape(n // 32, 32, m)
    amax = np.abs(b).max(1)
    byte = np.clip(np.where(amax > 0, np.frexp(amax)[1] - 1 + 127 - 7, 1), 1, 254)
    codes = (b * np.exp2(127.0 - byte)[:, None, :]).reshape(n, m).astype(np.float32).astype(ml_dtypes.float8_e4m3fn).view(np.uint8)
    words = codes.reshape(n // 512, 128, 4, m).transpose(0, 1, 3, 2)
    return np.ascontiguousarray(words), np.ascontiguousarray(byte.astype(np.uint8).reshape(n // 512, 16, m))


K, T, S, H, N = 1024, 2048, 1024, 512, 384

def setup_inputs():
    n = np.random.standard_normal
    s = mx_kscale(K)[:, None]
    u = mx_kscale(H)[:, None]
    tab_words, tab_scales = pack_weight(n((K, T)) * s, "e4m3")
    w2_words, w2_scales = pack_weight(n((K, H)) / np.sqrt(K) / s, "e2m1")
    w3_words, w3_scales = pack_weight(n((K, H)) / np.sqrt(K) / s, "e4m3")
    w5_words, w5_scales = pack_weight(n((K, N)) / np.sqrt(K) / s, "e2m1")
    return {
        "tab_words": tab_words, "tab_scales": tab_scales,
        "offs": striped(np.random.permutation(T)[:S]),
        "w1": (n((K, H)) / np.sqrt(K) / s * u.T).astype(np.float32),
        "w2_words": w2_words, "w2_scales": w2_scales,
        "w3_words": w3_words, "w3_scales": w3_scales,
        "w4": (n((H, N)) / np.sqrt(H) / u).astype(np.float32),
        "w5_words": w5_words, "w5_scales": w5_scales,
        "eff": np.random.uniform(0.3, 1.0, (N, S)).astype(np.float32),
    }

def reference(tab_words, tab_scales, offs, w1, w2_words, w2_scales, w3_words, w3_scales,
              w4, w5_words, w5_scales, eff):
    v = unpack_weight(tab_words, tab_scales, "e4m3")[:, unstriped(offs)]
    w2 = unpack_weight(w2_words, w2_scales, "e2m1")
    w3 = unpack_weight(w3_words, w3_scales, "e4m3")
    w5 = unpack_weight(w5_words, w5_scales, "e2m1")
    d1 = mxq(f64(w1), 0, "e4m3").T @ v
    d2 = w2.T @ v
    d3 = w3.T @ v
    h = d1 * d2 * d3
    words, scales = planes(h)
    hq = mxq(h, 0, "e4m3")
    triple = mxq(f64(w4), 0, "e4m3").T @ hq
    single = w5.T @ v
    y = triple + f64(eff) * single
    return y, h, words, scales

@@ -1,0 +1,306 @@
+from contextlib import ExitStack
+
+import concourse.mybir as mybir
+
+K, T, S, H, N = 1024, 2048, 1024, 512, 384
+FLOPS = 2 * S * (3 * K * H + H * N + K * N)
+
+F32 = mybir.dt.float32
+BF16 = mybir.dt.bfloat16
+I32 = mybir.dt.int32
+U32 = mybir.dt.uint32
+U16 = mybir.dt.uint16
+U8 = mybir.dt.uint8
+FP8X4 = mybir.dt.float8_e4m3fn_x4
+FP4X4 = mybir.dt.float4_e2m1fn_x4
+MULT = mybir.AluOpType.mult
+ADD = mybir.AluOpType.add
+
+P = 128
+PACK = 4
+PASSES = K // (P * PACK)
+HALF = 512
+BANK = 512
+NT = N // P
+CHUNKS = ((0, 256), (256, 256), (512, 256), (768, 128), (896, 128))
+
+
+def tile_list_photon_triple_coincidence_kernel(
+    tc, tab_words, tab_scales, offs, w1, w2_words, w2_scales, w3_words, w3_scales,
+    w4, w5_words, w5_scales, eff, out_0, out_1, out_2, out_3,
+):
+    nc = tc.nc
+    with ExitStack() as ctx:
+        keep = ctx.enter_context(tc.tile_pool(name="keep", bufs=1))
+        ring = ctx.enter_context(tc.tile_pool(name="ring", bufs=3))
+        psum = ctx.enter_context(tc.psum_pool(name="psum", bufs=8))
+
+        def held(name, shape, dtype):
+            return keep.tile(shape, dtype, name=name, align_bytes=64)
+
+        offsets = keep.tile([P, S // 16], U16, name="offsets")
+        tab_s = held("tab_s", [P, T], U8)
+        tab_w = [held("tab_w%d" % a, [P, T], U32) for a in range(PASSES)]
+        w2_s_raw = held("w2_s_raw", [P, PASSES * H], U8)
+        w3_s_raw = held("w3_s_raw", [P, H], U8)
+        w5_s = held("w5_s", [P, PASSES * N], U8)
+        v_s0 = held("v_s0", [P, S], U8)
+        v_s1 = held("v_s1", [P, S], U8)
+        w3_raw = held("w3_raw", [P, PASSES * H], I32)
+        w2_raw = held("w2_raw", [P, PASSES * H * 2], U8)
+        w5_w = held("w5_w", [P, PASSES * N * 2], U8)
+
+        nc.vector.memset(tab_s[:].bitcast(I32), 0)
+        nc.gpsimd.memset(w2_s_raw[:].bitcast(I32), 0)
+        nc.gpsimd.memset(w3_s_raw[:].bitcast(I32), 0)
+        nc.vector.memset(w5_s[:].bitcast(I32), 0)
+        nc.vector.memset(v_s1[:].bitcast(I32), 0)
+
+        def load_planes_side_by_side(tile, scales):
+            for q in range(4):
+                nc.sync.dma_start(
+                    tile[32 * q : 32 * q + 4, :].bitcast(I32).rearrange("r (a c) -> r a c", a=PASSES),
+                    scales[:, 4 * q : 4 * q + 4, :].rearrange("a r c -> r a c").bitcast(I32))
+
+        def load_planes_stacked(tile, scales):
+            for q in range(4):
+                nc.sync.dma_start(tile[32 * q : 32 * q + 8, :].bitcast(I32), scales[:, 4 * q : 4 * q + 4, :].bitcast(I32))
+
+        nc.sync.dma_start(offsets[:], offs)
+        load_planes_stacked(tab_s, tab_scales)
+        nc.sync.dma_start(tab_w[0][:].bitcast(I32), tab_words[0].rearrange("p t i -> p (t i)").bitcast(I32))
+        nc.sync.dma_start(
+            w3_raw[:].rearrange("p (a c) -> p a c", a=PASSES),
+            w3_words.rearrange("a p c i -> p a (c i)").bitcast(I32))
+        nc.sync.dma_start(
+            w2_raw[:].bitcast(I32).rearrange("p (a c) -> p a c", a=PASSES),
+            w2_words.rearrange("a p c -> p a c").bitcast(I32))
+        load_planes_stacked(w3_s_raw, w3_scales)
+        nc.sync.dma_start(tab_w[1][:].bitcast(I32), tab_words[1].rearrange("p t i -> p (t i)").bitcast(I32))
+        load_planes_side_by_side(w2_s_raw, w2_scales)
+        w1_raw = {}
+        for a in range(PASSES):
+            rows = w1[a * 512 : (a + 1) * 512, :].rearrange("(p j) c -> p j c", j=PACK)
+            for b in range(2):
+                w1_raw[a, b] = held("w1_raw%d%d" % (a, b), [P, PACK, H // 2], F32)
+                nc.sync.dma_start(w1_raw[a, b][:], rows[:, :, b * 256 : (b + 1) * 256])
+        nc.sync.dma_start(
+            w5_w[:].bitcast(I32).rearrange("p (a c) -> p a c", a=PASSES),
+            w5_words.rearrange("a p c -> p a c").bitcast(I32))
+        eff_sb = [held("eff%d" % hf, [P, NT, HALF], F32) for hf in range(2)]
+
+        def load_eff(hf):
+            nc.sync.dma_start(eff_sb[hf][:], eff[:, hf * HALF : (hf + 1) * HALF].rearrange("(i p) j -> p i j", p=P))
+
+        load_eff(0)
+        load_planes_side_by_side(w5_s, w5_scales)
+        w4_raw = held("w4_raw", [P, PACK, N], F32)
+        nc.sync.dma_start(w4_raw[:], w4.rearrange("(p j) n -> p j n", j=PACK))
+        load_eff(1)
+
+        nc.vector.tensor_copy(v_s0[:], tab_s[:].indirect(offsets[:]))
+        nc.scalar.dma_start(v_s1[0 : P - 4, :].bitcast(I32), v_s0[4:P, :].bitcast(I32))
+        v_s = [v_s0, v_s1]
+        v_w = {}
+
+        def gather(a, hf):
+            v_w[a, hf] = held("v_w%d%d" % (a, hf), [P, HALF], U32)
+            nc.vector.tensor_copy(v_w[a, hf][:], tab_w[a][:].indirect(offsets[:, hf * 32 : (hf + 1) * 32]))
+
+        gather(0, 0)
+        gather(0, 1)
+        w3_w = held("w3_w", [P, PACK * PASSES * P], I32)
+        nc.vector.tensor_copy(
+            w3_w[:].rearrange("p (t g i) -> p g t i", t=PACK, i=4),
+            w3_raw[:].rearrange("p (g i t) -> p g t i", t=PACK, i=4))
+        w2_w = held("w2_w", [P, PACK * PASSES * P * 2], U8)
+        nc.vector.tensor_copy(
+            w2_w[:].bitcast(U16).rearrange("p (t g i) -> p g t i", t=PACK, i=8),
+            w2_raw[:].bitcast(U16).rearrange("p (g i t) -> p g t i", t=PACK, i=8))
+        w3_s = held("w3_s", [P, PACK * P], U8)
+        nc.vector.tensor_copy(
+            w3_s[:].rearrange("p (t g i) -> p g t i", t=PACK, i=16),
+            w3_s_raw[:].rearrange("p (g i t) -> p g t i", t=PACK, i=16))
+        gather(1, 0)
+        w2_s = held("w2_s", [P, PACK * PASSES * P], U8)
+        nc.vector.tensor_copy(
+            w2_s[:].rearrange("p (t g i) -> p g t i", t=PACK, i=16),
+            w2_s_raw[:].rearrange("p (g i t) -> p g t i", t=PACK, i=16))
+        gather(1, 1)
+
+        def cols(t, a, width):
+            return slice((t * PASSES + a) * width, (t * PASSES + a + 1) * width)
+
+        w1_b = [held("w1_b%d" % a, [P, PACK * H], BF16) for a in range(PASSES)]
+        w1_w = [held("w1_w%d" % a, [P, H], U32) for a in range(PASSES)]
+        w1_s = [held("w1_s%d" % a, [P, H], U8) for a in range(PASSES)]
+
+        def round_on_scalar(dst, src):
+            nc.scalar.copy(dst, src)
+
+        def round_on_gpsimd(dst, src):
+            nc.gpsimd.tensor_scalar(dst, src, 1.0, 0.0, MULT, ADD)
+
+        def round_w1(a, b, how):
+            how(
+                w1_b[a][:].rearrange("p (t m j) -> p m t j", t=PACK, j=PACK)[:, b * 64 : (b + 1) * 64],
+                w1_raw[a, b][:].rearrange("p j (m t) -> p m t j", t=PACK))
+
+        def quantize_w1(a):
+            nc.vector.quantize_mx(out=w1_w[a][:].bitcast(FP8X4), scales=w1_s[a][:], in_=w1_b[a][:])
+
+        d23 = [held("d23_%d" % hf, [P, PACK, HALF], F32) for hf in range(2)]
+
+        def pass_w2(bank, t, a, hf):
+            nc.tensor.matmul_mx(
+                out=bank[:], lhsT=w2_w[:, cols(t, a, 2 * P)].bitcast(FP4X4), lhsT_scale=w2_s[:, cols(t, a, P)],
+                rhs=v_w[a, hf][:].bitcast(FP8X4), rhs_scale=v_s[a][:, hf * HALF : (hf + 1) * HALF],
+                start=(a == 0), stop=(a == PASSES - 1))
+
+        def pass_w3(bank, t, a, hf):
+            nc.tensor.matmul_mx(
+                out=bank[:], lhsT=w3_w[:, cols(t, a, P)].bitcast(FP8X4),
+                lhsT_scale=w3_s[4 * a : P, t * P : (t + 1) * P],
+                rhs=v_w[a, hf][:].bitcast(FP8X4), rhs_scale=v_s0[4 * a : P, hf * HALF : (hf + 1) * HALF],
+                start=(a == 0), stop=(a == PASSES - 1))
+
+        def multiply_23(b2, b3, t, hf):
+            d3 = ring.tile([P, HALF], F32, name="d3")
+            nc.scalar.copy(d3[:], b3[:])
+            nc.vector.tensor_tensor(d23[hf][:, t, :], b2[:], d3[:], MULT)
+
+        def stage1_first():
+            b3 = [psum.tile([P, HALF], F32, name="bank") for t in range(PACK)]
+            b2 = [psum.tile([P, HALF], F32, name="bank") for t in range(PACK)]
+            for a in range(PASSES):
+                for t in range(PACK):
+                    pass_w3(b3[t], t, a, 0)
+            for t in range(PACK):
+                for a in range(PASSES):
+                    pass_w2(b2[t], t, a, 0)
+                multiply_23(b2[t], b3[t], t, 0)
+
+        def stage1_second():
+            for t in range(PACK):
+                b3 = psum.tile([P, HALF], F32, name="bank")
+                b2 = psum.tile([P, HALF], F32, name="bank")
+                for a in range(PASSES):
+                    pass_w3(b3, t, a, 1)
+                for a in range(PASSES):
+                    pass_w2(b2, t, a, 1)
+                multiply_23(b2, b3, t, 1)
+
+        round_w1(0, 0, round_on_scalar)
+        stage1_first()
+        round_w1(0, 1, round_on_scalar)
+        quantize_w1(0)
+        round_w1(1, 0, round_on_scalar)
+        round_w1(1, 1, round_on_scalar)
+        stage1_second()
+        quantize_w1(1)
+
+        w4_b = held("w4_b", [P, N * PACK], BF16)
+        w4_w = held("w4_w", [P, N], U32)
+        w4_s = held("w4_s", [P, N], U8)
+        round_on_gpsimd(
+            w4_b[:].rearrange("p (c i j) -> p c j i", i=4, j=PACK),
+            w4_raw[:].rearrange("p j (c i) -> p c j i", i=4))
+
+        def quantize_w4():
+            for lo, hi in ((0, 256), (256, N)):
+                nc.vector.quantize_mx(out=w4_w[:, lo:hi].bitcast(FP8X4), scales=w4_s[:, lo:hi], in_=w4_b[:, PACK * lo : PACK * hi])
+
+        h_w = [held("h_w%d" % hf, [P, HALF], U32) for hf in range(2)]
+        h_s = held("h_s", [P, S], U8)
+        gated = [held("gated%d" % hf, [P, NT, HALF], F32) for hf in range(2)]
+        h_b = {}
+
+        def single(hf, i):
+            hcols = slice(hf * HALF, (hf + 1) * HALF)
+            bank = psum.tile([P, HALF], F32, name="bank")
+            for a in range(PASSES):
+                nc.tensor.matmul_mx(
+                    out=bank[:],
+                    lhsT=w5_w[:, 2 * (a * N + i * P) : 2 * (a * N + (i + 1) * P)].bitcast(FP4X4),
+                    lhsT_scale=w5_s[:, a * N + i * P : a * N + (i + 1) * P],
+                    rhs=v_w[a, hf][:].bitcast(FP8X4), rhs_scale=v_s[a][:, hcols],
+                    start=(a == 0), stop=(a == PASSES - 1))
+            lin = ring.tile([P, HALF], F32, name="lin")
+            nc.scalar.copy(lin[:], bank[:])
+            nc.gpsimd.tensor_tensor(gated[hf][:, i, :], lin[:], eff_sb[hf][:, i, :], MULT)
+
+        def make_h(c):
+            j0, width = CHUNKS[c]
+            hf, lo = j0 // HALF, j0 % HALF
+            per_bank = BANK // width
+            h = held("h%d" % c, [P, PACK, width], F32)
+            for t0 in range(0, PACK, per_bank):
+                bank = psum.tile([P, per_bank, width], F32, name="bank")
+                for e in range(per_bank):
+                    t = t0 + e
+                    for a in range(PASSES):
+                        nc.tensor.matmul_mx(
+                            out=bank[:, e, :], lhsT=w1_w[a][:, t * P : (t + 1) * P].bitcast(FP8X4),
+                            lhsT_scale=w1_s[a][:, t * P : (t + 1) * P],
+                            rhs=v_w[a, hf][:, lo : lo + width].bitcast(FP8X4),
+                            rhs_scale=v_s[a][:, j0 : j0 + width],
+                            start=(a == 0), stop=(a == PASSES - 1))
+                nc.vector.tensor_tensor(
+                    h[:, t0 : t0 + per_bank, :], bank[:], d23[hf][:, t0 : t0 + per_bank, lo : lo + width], MULT)
+            h_b[c] = held("h_b%d" % c, [P, width * PACK], BF16)
+            nc.scalar.copy(
+                h_b[c][:].rearrange("p (c i t) -> p c t i", i=4, t=PACK),
+                h[:].rearrange("p t (c i) -> p c t i", i=4))
+            nc.sync.dma_start(out_1[:, j0 : j0 + width].rearrange("(p t) j -> p t j", t=PACK), h[:])
+
+        def quantize_h(c):
+            j0, width = CHUNKS[c]
+            hf, lo = j0 // HALF, j0 % HALF
+            nc.vector.quantize_mx(
+                out=h_w[hf][:, lo : lo + width].bitcast(FP8X4), scales=h_s[:, j0 : j0 + width], in_=h_b[c][:])
+            if lo + width == HALF:
+                nc.sync.dma_start(
+                    out_2[0, :, hf * HALF : (hf + 1) * HALF, :].rearrange("p m t -> p (m t)").bitcast(I32),
+                    h_w[hf][:].bitcast(I32))
+
+        def finish(c):
+            j0, width = CHUNKS[c]
+            hf, lo = j0 // HALF, j0 % HALF
+            per_bank = BANK // width
+            y = held("y%d" % c, [P, NT, width], F32)
+            for i0 in range(0, NT, per_bank):
+                i1 = min(i0 + per_bank, NT)
+                bank = psum.tile([P, per_bank, width], F32, name="bank")
+                for i in range(i0, i1):
+                    nc.tensor.matmul_mx(
+                        out=bank[:, i - i0, :], lhsT=w4_w[:, i * P : (i + 1) * P].bitcast(FP8X4),
+                        lhsT_scale=w4_s[:, i * P : (i + 1) * P],
+                        rhs=h_w[hf][:, lo : lo + width].bitcast(FP8X4),
+                        rhs_scale=h_s[:, j0 : j0 + width], start=True, stop=True)
+                nc.vector.tensor_tensor(
+                    y[:, i0:i1, :], bank[:, 0 : i1 - i0, :], gated[hf][:, i0:i1, lo : lo + width], ADD)
+            nc.sync.dma_start(out_0[:, j0 : j0 + width].rearrange("(i p) j -> p i j", p=P), y[:])
+
+        for i in range(NT):
+            single(0, i)
+        make_h(0)
+        quantize_w4()
+        make_h(1)
+        quantize_h(0)
+        single(1, 0)
+        finish(0)
+        make_h(2)
+        quantize_h(1)
+        single(1, 1)
+        single(1, 2)
+        finish(1)
+        make_h(3)
+        quantize_h(2)
+        make_h(4)
+        finish(2)
+        quantize_h(3)
+        finish(3)
+        quantize_h(4)
+        for q in range(4):
+            nc.scalar.dma_start(out_3[0, 4 * q : 4 * q + 4, :].bitcast(I32), h_s[32 * q : 32 * q + 4, :].bitcast(I32))
+        finish(len(CHUNKS) - 1)

@@ -66,67 +66,77 @@ def tile_list_photon_triple_coincidence_kernel(
             for q in range(4):
                 nc.sync.dma_start(tile[32 * q : 32 * q + 8, :].bitcast(I32), scales[:, 4 * q : 4 * q + 4, :].bitcast(I32))
 
-        nc.sync.dma_start(offsets[:], offs)
-        load_planes_stacked(tab_s, tab_scales)
-        nc.sync.dma_start(tab_w[0][:].bitcast(I32), tab_words[0].rearrange("p t i -> p (t i)").bitcast(I32))
-        nc.sync.dma_start(
-            w3_raw[:].rearrange("p (a c) -> p a c", a=PASSES),
-            w3_words.rearrange("a p c i -> p a (c i)").bitcast(I32))
-        nc.sync.dma_start(
-            w2_raw[:].bitcast(I32).rearrange("p (a c) -> p a c", a=PASSES),
-            w2_words.rearrange("a p c -> p a c").bitcast(I32))
-        load_planes_stacked(w3_s_raw, w3_scales)
-        nc.sync.dma_start(tab_w[1][:].bitcast(I32), tab_words[1].rearrange("p t i -> p (t i)").bitcast(I32))
-        load_planes_side_by_side(w2_s_raw, w2_scales)
+        def load_words(tile, words):
+            nc.sync.dma_start(tile[:].bitcast(I32).rearrange("p (a c) -> p a c", a=PASSES), words.bitcast(I32))
+
+        def load_words_pass(tile, words, a):
+            nc.sync.dma_start(tile[:, a * H : (a + 1) * H], words[a].rearrange("p c i -> p (c i)").bitcast(I32))
+
+        def load_table(a):
+            nc.sync.dma_start(tab_w[a][:].bitcast(I32), tab_words[a].rearrange("p t i -> p (t i)").bitcast(I32))
+
         w1_raw = {}
-        for a in range(PASSES):
+
+        def load_w1(a, b):
             rows = w1[a * 512 : (a + 1) * 512, :].rearrange("(p j) c -> p j c", j=PACK)
-            for b in range(2):
-                w1_raw[a, b] = held("w1_raw%d%d" % (a, b), [P, PACK, H // 2], F32)
-                nc.sync.dma_start(w1_raw[a, b][:], rows[:, :, b * 256 : (b + 1) * 256])
-        nc.sync.dma_start(
-            w5_w[:].bitcast(I32).rearrange("p (a c) -> p a c", a=PASSES),
-            w5_words.rearrange("a p c -> p a c").bitcast(I32))
+            w1_raw[a, b] = held("w1_raw%d%d" % (a, b), [P, PACK, H // 2], F32)
+            nc.sync.dma_start(w1_raw[a, b][:], rows[:, :, b * 256 : (b + 1) * 256])
+
         eff_sb = [held("eff%d" % hf, [P, NT, HALF], F32) for hf in range(2)]
 
         def load_eff(hf):
             nc.sync.dma_start(eff_sb[hf][:], eff[:, hf * HALF : (hf + 1) * HALF].rearrange("(i p) j -> p i j", p=P))
 
-        load_eff(0)
-        load_planes_side_by_side(w5_s, w5_scales)
         w4_raw = held("w4_raw", [P, PACK, N], F32)
+
+        nc.sync.dma_start(offsets[:], offs)
+        load_words_pass(w3_raw, w3_words, 0)
+        load_words_pass(w3_raw, w3_words, 1)
+        load_planes_stacked(tab_s, tab_scales)
+        load_table(0)
+        load_planes_stacked(w3_s_raw, w3_scales)
+        load_table(1)
+        load_words(w2_raw, w2_words.rearrange("a p c -> p a c"))
+        load_planes_side_by_side(w2_s_raw, w2_scales)
+        load_w1(0, 0)
+        load_w1(0, 1)
+        load_w1(1, 0)
+        load_w1(1, 1)
+        load_words(w5_w, w5_words.rearrange("a p c -> p a c"))
+        load_planes_side_by_side(w5_s, w5_scales)
         nc.sync.dma_start(w4_raw[:], w4.rearrange("(p j) n -> p j n", j=PACK))
+        load_eff(0)
         load_eff(1)
 
-        nc.vector.tensor_copy(v_s0[:], tab_s[:].indirect(offsets[:]))
-        nc.scalar.dma_start(v_s1[0 : P - 4, :].bitcast(I32), v_s0[4:P, :].bitcast(I32))
         v_s = [v_s0, v_s1]
         v_w = {}
+        w3_w = held("w3_w", [P, PACK * PASSES * P], I32)
+        w2_w = held("w2_w", [P, PACK * PASSES * P * 2], U8)
+        w3_s = held("w3_s", [P, PACK * P], U8)
+        w2_s = held("w2_s", [P, PACK * PASSES * P], U8)
+
+        def deal(dst, src, run):
+            nc.vector.tensor_copy(
+                dst.rearrange("p (t g i) -> p g t i", t=PACK, i=run),
+                src.rearrange("p (g i t) -> p g t i", t=PACK, i=run))
 
         def gather(a, hf):
             v_w[a, hf] = held("v_w%d%d" % (a, hf), [P, HALF], U32)
             nc.vector.tensor_copy(v_w[a, hf][:], tab_w[a][:].indirect(offsets[:, hf * 32 : (hf + 1) * 32]))
 
+        def gather_scales():
+            nc.vector.tensor_copy(v_s0[:], tab_s[:].indirect(offsets[:]))
+            nc.scalar.dma_start(v_s1[0:112, :].bitcast(I32), v_s0[4:116, :].bitcast(I32))
+
+        deal(w3_w[:], w3_raw[:], 4)
+        gather_scales()
         gather(0, 0)
+        deal(w3_s[:], w3_s_raw[:], 16)
         gather(0, 1)
-        w3_w = held("w3_w", [P, PACK * PASSES * P], I32)
-        nc.vector.tensor_copy(
-            w3_w[:].rearrange("p (t g i) -> p g t i", t=PACK, i=4),
-            w3_raw[:].rearrange("p (g i t) -> p g t i", t=PACK, i=4))
-        w2_w = held("w2_w", [P, PACK * PASSES * P * 2], U8)
-        nc.vector.tensor_copy(
-            w2_w[:].bitcast(U16).rearrange("p (t g i) -> p g t i", t=PACK, i=8),
-            w2_raw[:].bitcast(U16).rearrange("p (g i t) -> p g t i", t=PACK, i=8))
-        w3_s = held("w3_s", [P, PACK * P], U8)
-        nc.vector.tensor_copy(
-            w3_s[:].rearrange("p (t g i) -> p g t i", t=PACK, i=16),
-            w3_s_raw[:].rearrange("p (g i t) -> p g t i", t=PACK, i=16))
         gather(1, 0)
-        w2_s = held("w2_s", [P, PACK * PASSES * P], U8)
-        nc.vector.tensor_copy(
-            w2_s[:].rearrange("p (t g i) -> p g t i", t=PACK, i=16),
-            w2_s_raw[:].rearrange("p (g i t) -> p g t i", t=PACK, i=16))
         gather(1, 1)
+        deal(w2_w[:].bitcast(U16), w2_raw[:].bitcast(U16), 8)
+        deal(w2_s[:], w2_s_raw[:], 16)
 
         def cols(t, a, width):
             return slice((t * PASSES + a) * width, (t * PASSES + a + 1) * width)
@@ -137,6 +147,9 @@ def tile_list_photon_triple_coincidence_kernel(
 
         def round_on_scalar(dst, src):
             nc.scalar.copy(dst, src)
+
+        def round_on_vector(dst, src):
+            nc.vector.tensor_copy(dst, src)
 
         def round_on_gpsimd(dst, src):
             nc.gpsimd.tensor_scalar(dst, src, 1.0, 0.0, MULT, ADD)
@@ -164,47 +177,48 @@ def tile_list_photon_triple_coincidence_kernel(
                 rhs=v_w[a, hf][:].bitcast(FP8X4), rhs_scale=v_s0[4 * a : P, hf * HALF : (hf + 1) * HALF],
                 start=(a == 0), stop=(a == PASSES - 1))
 
-        def multiply_23(b2, b3, t, hf):
-            d3 = ring.tile([P, HALF], F32, name="d3")
-            nc.scalar.copy(d3[:], b3[:])
-            nc.vector.tensor_tensor(d23[hf][:, t, :], b2[:], d3[:], MULT)
+        banks_3 = {}
+        d3 = {}
 
-        def stage1_first():
-            b3 = [psum.tile([P, HALF], F32, name="bank") for t in range(PACK)]
-            b2 = [psum.tile([P, HALF], F32, name="bank") for t in range(PACK)]
-            for a in range(PASSES):
+        def products_3():
+            for hf in range(2):
                 for t in range(PACK):
-                    pass_w3(b3[t], t, a, 0)
-            for t in range(PACK):
-                for a in range(PASSES):
-                    pass_w2(b2[t], t, a, 0)
-                multiply_23(b2[t], b3[t], t, 0)
+                    banks_3[t, hf] = psum.tile([P, HALF], F32, name="bank")
+            for a in range(PASSES):
+                for hf in range(2):
+                    for t in range(PACK):
+                        pass_w3(banks_3[t, hf], t, a, hf)
 
-        def stage1_second():
-            for t in range(PACK):
-                b3 = psum.tile([P, HALF], F32, name="bank")
-                b2 = psum.tile([P, HALF], F32, name="bank")
-                for a in range(PASSES):
-                    pass_w3(b3, t, a, 1)
-                for a in range(PASSES):
-                    pass_w2(b2, t, a, 1)
-                multiply_23(b2, b3, t, 1)
+        def copy_3(t, hf):
+            d3[t, hf] = held("d3_%d%d" % (t, hf), [P, HALF], F32)
+            nc.scalar.copy(d3[t, hf][:], banks_3[t, hf][:])
 
-        round_w1(0, 0, round_on_scalar)
-        stage1_first()
-        round_w1(0, 1, round_on_scalar)
-        quantize_w1(0)
-        round_w1(1, 0, round_on_scalar)
-        round_w1(1, 1, round_on_scalar)
-        stage1_second()
-        quantize_w1(1)
+        def product_2(t, hf):
+            bank = psum.tile([P, HALF], F32, name="bank")
+            for a in range(PASSES):
+                pass_w2(bank, t, a, hf)
+            nc.vector.tensor_tensor(d23[hf][:, t, :], bank[:], d3[t, hf][:], MULT)
 
         w4_b = held("w4_b", [P, N * PACK], BF16)
         w4_w = held("w4_w", [P, N], U32)
         w4_s = held("w4_s", [P, N], U8)
-        round_on_gpsimd(
-            w4_b[:].rearrange("p (c i j) -> p c j i", i=4, j=PACK),
-            w4_raw[:].rearrange("p j (c i) -> p c j i", i=4))
+
+        def round_w4(how):
+            how(
+                w4_b[:].rearrange("p (c i j) -> p c j i", i=4, j=PACK),
+                w4_raw[:].rearrange("p j (c i) -> p c j i", i=4))
+
+        W4_PARTS = ((0, 256), (256, N))
+
+        def round_w4_part(k, how):
+            lo, hi = W4_PARTS[k]
+            how(
+                w4_b[:, PACK * lo : PACK * hi].rearrange("p (c i j) -> p c j i", i=4, j=PACK),
+                w4_raw[:, :, lo:hi].rearrange("p j (c i) -> p c j i", i=4))
+
+        def quantize_w4_part(k):
+            lo, hi = W4_PARTS[k]
+            nc.vector.quantize_mx(out=w4_w[:, lo:hi].bitcast(FP8X4), scales=w4_s[:, lo:hi], in_=w4_b[:, PACK * lo : PACK * hi])
 
         def quantize_w4():
             for lo, hi in ((0, 256), (256, N)):
@@ -281,24 +295,51 @@ def tile_list_photon_triple_coincidence_kernel(
                     y[:, i0:i1, :], bank[:, 0 : i1 - i0, :], gated[hf][:, i0:i1, lo : lo + width], ADD)
             nc.sync.dma_start(out_0[:, j0 : j0 + width].rearrange("(i p) j -> p i j", p=P), y[:])
 
-        for i in range(NT):
-            single(0, i)
+        products_3()
+        round_w1(0, 0, round_on_scalar)
+        copy_3(0, 0)
+        copy_3(1, 0)
+        round_w1(0, 1, round_on_vector)
+        copy_3(2, 0)
+        product_2(0, 0)
+        quantize_w1(0)
+        copy_3(3, 0)
+        product_2(1, 0)
+        round_w1(1, 0, round_on_scalar)
+        product_2(2, 0)
+        round_w1(1, 1, round_on_vector)
+        product_2(3, 0)
+        copy_3(0, 1)
+        copy_3(1, 1)
+        quantize_w1(1)
+        product_2(0, 1)
+        copy_3(2, 1)
+        product_2(1, 1)
+        copy_3(3, 1)
+        product_2(2, 1)
+        product_2(3, 1)
+        single(0, 0)
+        single(0, 1)
         make_h(0)
-        quantize_w4()
+        round_w4_part(0, round_on_scalar)
+        single(0, 2)
         make_h(1)
+        round_w4_part(1, round_on_scalar)
         quantize_h(0)
+        quantize_w4_part(0)
+        quantize_w4_part(1)
         single(1, 0)
-        finish(0)
         make_h(2)
         quantize_h(1)
+        finish(0)
         single(1, 1)
-        single(1, 2)
-        finish(1)
         make_h(3)
-        quantize_h(2)
+        single(1, 2)
         make_h(4)
-        finish(2)
+        finish(1)
+        quantize_h(2)
         quantize_h(3)
+        finish(2)
         finish(3)
         quantize_h(4)
         for q in range(4):

@@ -22,7 +22,9 @@ PASSES = K // (P * PACK)
 HALF = 512
 BANK = 512
 NT = N // P
-CHUNKS = ((0, 256), (256, 256), (512, 256), (768, 128), (896, 128))
+D3_PLACE = {(0, 0): "piece00", (0, 1): "piece01", (1, 0): "piece10", (1, 1): "piece11"}
+D23_PLACE = {(0, 0): "d23_00", (0, 1): "d23_01", (1, 0): "d23_10", (1, 1): "d23_11"}
+CHUNKS = ((0, 256), (256, 256), (512, 256), (768, 256))
 
 
 def tile_list_photon_triple_coincidence_kernel(
@@ -36,25 +38,25 @@ def tile_list_photon_triple_coincidence_kernel(
         psum = ctx.enter_context(tc.psum_pool(name="psum", bufs=8))
 
         def held(name, shape, dtype):
-            return keep.tile(shape, dtype, name=name, align_bytes=64)
+            return keep.tile(shape, dtype, name=name, align_bytes=256)
+
+        def shared(name, tag, shape):
+            return keep.tile(shape, F32, name=name, tag=tag, align_bytes=256)
 
         offsets = keep.tile([P, S // 16], U16, name="offsets")
         tab_s = held("tab_s", [P, T], U8)
         tab_w = [held("tab_w%d" % a, [P, T], U32) for a in range(PASSES)]
-        w2_s_raw = held("w2_s_raw", [P, PASSES * H], U8)
-        w3_s_raw = held("w3_s_raw", [P, H], U8)
+        w2_s_raw = keep.tile([P, PASSES * H], U8, name="w2_s_raw", tag="picked11", align_bytes=256)
+        w3_s_raw = keep.tile([P, H], U8, name="w3_s_raw", tag="picked01", align_bytes=256)
         w5_s = held("w5_s", [P, PASSES * N], U8)
-        v_s0 = held("v_s0", [P, S], U8)
         v_s1 = held("v_s1", [P, S], U8)
         w3_raw = held("w3_raw", [P, PASSES * H], I32)
-        w2_raw = held("w2_raw", [P, PASSES * H * 2], U8)
+        w2_raw = keep.tile([P, PASSES * H * 2], U8, name="w2_raw", tag="early", align_bytes=256)
+        v_s0 = keep.tile([P, S], U8, name="v_s0", tag="early", align_bytes=256)
         w5_w = held("w5_w", [P, PASSES * N * 2], U8)
 
-        nc.vector.memset(tab_s[:].bitcast(I32), 0)
-        nc.gpsimd.memset(w2_s_raw[:].bitcast(I32), 0)
-        nc.gpsimd.memset(w3_s_raw[:].bitcast(I32), 0)
-        nc.vector.memset(w5_s[:].bitcast(I32), 0)
-        nc.vector.memset(v_s1[:].bitcast(I32), 0)
+        for plane in (tab_s, w3_s_raw, w2_s_raw, v_s1, w5_s):
+            nc.vector.memset(plane[:].bitcast(I32), 0)
 
         def load_planes_side_by_side(tile, scales):
             for q in range(4):
@@ -79,7 +81,7 @@ def tile_list_photon_triple_coincidence_kernel(
 
         def load_w1(a, b):
             rows = w1[a * 512 : (a + 1) * 512, :].rearrange("(p j) c -> p j c", j=PACK)
-            w1_raw[a, b] = held("w1_raw%d%d" % (a, b), [P, PACK, H // 2], F32)
+            w1_raw[a, b] = shared("w1_raw%d%d" % (a, b), "piece%d%d" % (a, b), [P, PACK, H // 2])
             nc.sync.dma_start(w1_raw[a, b][:], rows[:, :, b * 256 : (b + 1) * 256])
 
         eff_sb = [held("eff%d" % hf, [P, NT, HALF], F32) for hf in range(2)]
@@ -89,14 +91,13 @@ def tile_list_photon_triple_coincidence_kernel(
 
         w4_raw = held("w4_raw", [P, PACK, N], F32)
 
+        load_words(w3_raw, w3_words.rearrange("a p c i -> p a (c i)"))
+        load_words(w2_raw, w2_words.rearrange("a p c -> p a c"))
         nc.sync.dma_start(offsets[:], offs)
-        load_words_pass(w3_raw, w3_words, 0)
-        load_words_pass(w3_raw, w3_words, 1)
         load_planes_stacked(tab_s, tab_scales)
         load_table(0)
         load_planes_stacked(w3_s_raw, w3_scales)
         load_table(1)
-        load_words(w2_raw, w2_words.rearrange("a p c -> p a c"))
         load_planes_side_by_side(w2_s_raw, w2_scales)
         load_w1(0, 0)
         load_w1(0, 1)
@@ -121,7 +122,7 @@ def tile_list_photon_triple_coincidence_kernel(
                 src.rearrange("p (g i t) -> p g t i", t=PACK, i=run))
 
         def gather(a, hf):
-            v_w[a, hf] = held("v_w%d%d" % (a, hf), [P, HALF], U32)
+            v_w[a, hf] = keep.tile([P, HALF], U32, name="v_w%d%d" % (a, hf), tag="picked%d%d" % (a, hf), align_bytes=256)
             nc.vector.tensor_copy(v_w[a, hf][:], tab_w[a][:].indirect(offsets[:, hf * 32 : (hf + 1) * 32]))
 
         def gather_scales():
@@ -129,14 +130,14 @@ def tile_list_photon_triple_coincidence_kernel(
             nc.scalar.dma_start(v_s1[0:112, :].bitcast(I32), v_s0[4:116, :].bitcast(I32))
 
         deal(w3_w[:], w3_raw[:], 4)
+        deal(w2_w[:].bitcast(U16), w2_raw[:].bitcast(U16), 8)
         gather_scales()
         gather(0, 0)
         deal(w3_s[:], w3_s_raw[:], 16)
         gather(0, 1)
         gather(1, 0)
-        gather(1, 1)
-        deal(w2_w[:].bitcast(U16), w2_raw[:].bitcast(U16), 8)
         deal(w2_s[:], w2_s_raw[:], 16)
+        gather(1, 1)
 
         def cols(t, a, width):
             return slice((t * PASSES + a) * width, (t * PASSES + a + 1) * width)
@@ -162,7 +163,7 @@ def tile_list_photon_triple_coincidence_kernel(
         def quantize_w1(a):
             nc.vector.quantize_mx(out=w1_w[a][:].bitcast(FP8X4), scales=w1_s[a][:], in_=w1_b[a][:])
 
-        d23 = [held("d23_%d" % hf, [P, PACK, HALF], F32) for hf in range(2)]
+        d23 = {}
 
         def pass_w2(bank, t, a, hf):
             nc.tensor.matmul_mx(
@@ -180,24 +181,24 @@ def tile_list_photon_triple_coincidence_kernel(
         banks_3 = {}
         d3 = {}
 
-        def products_3():
-            for hf in range(2):
-                for t in range(PACK):
+        def products_3(hf, a):
+            for t in range(PACK):
+                if a == 0:
                     banks_3[t, hf] = psum.tile([P, HALF], F32, name="bank")
-            for a in range(PASSES):
-                for hf in range(2):
-                    for t in range(PACK):
-                        pass_w3(banks_3[t, hf], t, a, hf)
+                pass_w3(banks_3[t, hf], t, a, hf)
 
         def copy_3(t, hf):
-            d3[t, hf] = held("d3_%d%d" % (t, hf), [P, HALF], F32)
-            nc.scalar.copy(d3[t, hf][:], banks_3[t, hf][:])
+            if t % 2 == 0:
+                d3[hf, t // 2] = shared("d3_%d%d" % (hf, t // 2), D3_PLACE[hf, t // 2], [P, 2, HALF])
+            nc.scalar.copy(d3[hf, t // 2][:, t % 2, :], banks_3[t, hf][:])
 
         def product_2(t, hf):
             bank = psum.tile([P, HALF], F32, name="bank")
             for a in range(PASSES):
                 pass_w2(bank, t, a, hf)
-            nc.vector.tensor_tensor(d23[hf][:, t, :], bank[:], d3[t, hf][:], MULT)
+            if t % 2 == 0:
+                d23[hf, t // 2] = shared("d23_%d%d" % (hf, t // 2), D23_PLACE[hf, t // 2], [P, 2, HALF])
+            nc.vector.tensor_tensor(d23[hf, t // 2][:, t % 2, :], bank[:], d3[hf, t // 2][:, t % 2, :], MULT)
 
         w4_b = held("w4_b", [P, N * PACK], BF16)
         w4_w = held("w4_w", [P, N], U32)
@@ -228,8 +229,19 @@ def tile_list_photon_triple_coincidence_kernel(
         h_s = held("h_s", [P, S], U8)
         gated = [held("gated%d" % hf, [P, NT, HALF], F32) for hf in range(2)]
         h_b = {}
+        h = [held("h%d" % hf, [P, PACK, HALF], F32) for hf in range(2)]
+        y = [held("y%d" % hf, [P, NT, HALF], F32) for hf in range(2)]
 
-        def single(hf, i):
+        def gate_on_gpsimd(bank, hf, i):
+            lin = ring.tile([P, HALF], F32, name="lin")
+            nc.scalar.copy(lin[:], bank[:])
+            for lo in range(0, HALF, 512):
+                nc.gpsimd.tensor_tensor(gated[hf][:, i, lo : lo + 512], lin[:, lo : lo + 512], eff_sb[hf][:, i, lo : lo + 512], MULT)
+
+        def gate_on_vector(bank, hf, i):
+            nc.vector.tensor_tensor(gated[hf][:, i, :], bank[:], eff_sb[hf][:, i, :], MULT)
+
+        def single(hf, i, gate):
             hcols = slice(hf * HALF, (hf + 1) * HALF)
             bank = psum.tile([P, HALF], F32, name="bank")
             for a in range(PASSES):
@@ -239,15 +251,12 @@ def tile_list_photon_triple_coincidence_kernel(
                     lhsT_scale=w5_s[:, a * N + i * P : a * N + (i + 1) * P],
                     rhs=v_w[a, hf][:].bitcast(FP8X4), rhs_scale=v_s[a][:, hcols],
                     start=(a == 0), stop=(a == PASSES - 1))
-            lin = ring.tile([P, HALF], F32, name="lin")
-            nc.scalar.copy(lin[:], bank[:])
-            nc.gpsimd.tensor_tensor(gated[hf][:, i, :], lin[:], eff_sb[hf][:, i, :], MULT)
+            gate(bank, hf, i)
 
         def make_h(c):
             j0, width = CHUNKS[c]
             hf, lo = j0 // HALF, j0 % HALF
             per_bank = BANK // width
-            h = held("h%d" % c, [P, PACK, width], F32)
             for t0 in range(0, PACK, per_bank):
                 bank = psum.tile([P, per_bank, width], F32, name="bank")
                 for e in range(per_bank):
@@ -260,28 +269,46 @@ def tile_list_photon_triple_coincidence_kernel(
                             rhs_scale=v_s[a][:, j0 : j0 + width],
                             start=(a == 0), stop=(a == PASSES - 1))
                 nc.vector.tensor_tensor(
-                    h[:, t0 : t0 + per_bank, :], bank[:], d23[hf][:, t0 : t0 + per_bank, lo : lo + width], MULT)
+                    h[hf][:, t0 : t0 + per_bank, lo : lo + width], bank[:],
+                    d23[hf, t0 // 2][:, :, lo : lo + width], MULT)
+
+        def round_h(c, how):
+            j0, width = CHUNKS[c]
+            hf, lo = j0 // HALF, j0 % HALF
             h_b[c] = held("h_b%d" % c, [P, width * PACK], BF16)
-            nc.scalar.copy(
+            how(
                 h_b[c][:].rearrange("p (c i t) -> p c t i", i=4, t=PACK),
-                h[:].rearrange("p t (c i) -> p c t i", i=4))
-            nc.sync.dma_start(out_1[:, j0 : j0 + width].rearrange("(p t) j -> p t j", t=PACK), h[:])
+                h[hf][:, :, lo : lo + width].rearrange("p t (c i) -> p c t i", i=4))
+
+        def store_h(j0, j1):
+            hf = j0 // HALF
+            nc.sync.dma_start(
+                out_1[:, j0:j1].rearrange("(p t) j -> p t j", t=PACK), h[hf][:, :, j0 - hf * HALF : j1 - hf * HALF])
+
+        def store_y(j0, j1):
+            hf = j0 // HALF
+            nc.sync.dma_start(
+                out_0[:, j0:j1].rearrange("(i p) j -> p i j", p=P), y[hf][:, :, j0 - hf * HALF : j1 - hf * HALF])
 
         def quantize_h(c):
             j0, width = CHUNKS[c]
             hf, lo = j0 // HALF, j0 % HALF
             nc.vector.quantize_mx(
                 out=h_w[hf][:, lo : lo + width].bitcast(FP8X4), scales=h_s[:, j0 : j0 + width], in_=h_b[c][:])
-            if lo + width == HALF:
-                nc.sync.dma_start(
-                    out_2[0, :, hf * HALF : (hf + 1) * HALF, :].rearrange("p m t -> p (m t)").bitcast(I32),
-                    h_w[hf][:].bitcast(I32))
 
-        def finish(c):
+        def store_codes(hf):
+            nc.sync.dma_start(
+                out_2[0, :, hf * HALF : (hf + 1) * HALF, :].rearrange("p m t -> p (m t)").bitcast(I32),
+                h_w[hf][:].bitcast(I32))
+
+        def store_scales():
+            for q in range(4):
+                nc.scalar.dma_start(out_3[0, 4 * q : 4 * q + 4, :].bitcast(I32), h_s[32 * q : 32 * q + 4, :].bitcast(I32))
+
+        def finish(c, store_each):
             j0, width = CHUNKS[c]
             hf, lo = j0 // HALF, j0 % HALF
             per_bank = BANK // width
-            y = held("y%d" % c, [P, NT, width], F32)
             for i0 in range(0, NT, per_bank):
                 i1 = min(i0 + per_bank, NT)
                 bank = psum.tile([P, per_bank, width], F32, name="bank")
@@ -292,56 +319,71 @@ def tile_list_photon_triple_coincidence_kernel(
                         rhs=h_w[hf][:, lo : lo + width].bitcast(FP8X4),
                         rhs_scale=h_s[:, j0 : j0 + width], start=True, stop=True)
                 nc.vector.tensor_tensor(
-                    y[:, i0:i1, :], bank[:, 0 : i1 - i0, :], gated[hf][:, i0:i1, lo : lo + width], ADD)
-            nc.sync.dma_start(out_0[:, j0 : j0 + width].rearrange("(i p) j -> p i j", p=P), y[:])
+                    y[hf][:, i0:i1, lo : lo + width], bank[:, 0 : i1 - i0, :], gated[hf][:, i0:i1, lo : lo + width], ADD)
+                if store_each:
+                    nc.sync.dma_start(
+                        out_0[i0 * P : i1 * P, j0 : j0 + width].rearrange("(i p) j -> p i j", p=P),
+                        y[hf][:, i0:i1, lo : lo + width])
 
-        products_3()
+        products_3(0, 0)
+        products_3(1, 0)
+        products_3(0, 1)
         round_w1(0, 0, round_on_scalar)
+        round_w1(0, 1, round_on_vector)
+        quantize_w1(0)
         copy_3(0, 0)
         copy_3(1, 0)
-        round_w1(0, 1, round_on_vector)
-        copy_3(2, 0)
         product_2(0, 0)
-        quantize_w1(0)
-        copy_3(3, 0)
         product_2(1, 0)
-        round_w1(1, 0, round_on_scalar)
+        products_3(1, 1)
+        copy_3(2, 0)
+        copy_3(3, 0)
         product_2(2, 0)
-        round_w1(1, 1, round_on_vector)
         product_2(3, 0)
+        round_w1(1, 0, round_on_scalar)
+        round_w1(1, 1, round_on_vector)
+        quantize_w1(1)
         copy_3(0, 1)
         copy_3(1, 1)
-        quantize_w1(1)
-        product_2(0, 1)
         copy_3(2, 1)
-        product_2(1, 1)
         copy_3(3, 1)
+        product_2(0, 1)
+        product_2(1, 1)
         product_2(2, 1)
         product_2(3, 1)
-        single(0, 0)
-        single(0, 1)
-        make_h(0)
         round_w4_part(0, round_on_scalar)
-        single(0, 2)
-        make_h(1)
         round_w4_part(1, round_on_scalar)
-        quantize_h(0)
+        make_h(0)
+        store_h(0, 256)
+        round_h(0, round_on_scalar)
+        make_h(1)
+        store_h(256, 512)
+        round_h(1, round_on_scalar)
         quantize_w4_part(0)
         quantize_w4_part(1)
-        single(1, 0)
-        make_h(2)
+        single(0, 0, gate_on_vector)
+        quantize_h(0)
+        single(0, 1, gate_on_vector)
+        single(0, 2, gate_on_vector)
         quantize_h(1)
-        finish(0)
-        single(1, 1)
+        store_codes(0)
+        make_h(2)
+        store_h(512, 768)
+        round_h(2, round_on_scalar)
+        finish(0, False)
+        store_y(0, 256)
         make_h(3)
-        single(1, 2)
-        make_h(4)
-        finish(1)
+        store_h(768, 1024)
+        round_h(3, round_on_scalar)
+        finish(1, False)
+        store_y(256, 512)
         quantize_h(2)
+        single(1, 0, gate_on_vector)
+        single(1, 1, gate_on_vector)
+        single(1, 2, gate_on_vector)
         quantize_h(3)
-        finish(2)
-        finish(3)
-        quantize_h(4)
-        for q in range(4):
-            nc.scalar.dma_start(out_3[0, 4 * q : 4 * q + 4, :].bitcast(I32), h_s[32 * q : 32 * q + 4, :].bitcast(I32))
-        finish(len(CHUNKS) - 1)
+        store_codes(1)
+        store_scales()
+        finish(2, False)
+        store_y(512, 768)
+        finish(3, True)

@@ -233,10 +233,10 @@ def tile_list_photon_triple_coincidence_kernel(
         y = [held("y%d" % hf, [P, NT, HALF], F32) for hf in range(2)]
 
         def gate_on_gpsimd(bank, hf, i):
-            lin = ring.tile([P, HALF], F32, name="lin")
+            lin = ring.tile([P, HALF], F32, name="lin", bufs=6)
             nc.scalar.copy(lin[:], bank[:])
-            for lo in range(0, HALF, 512):
-                nc.gpsimd.tensor_tensor(gated[hf][:, i, lo : lo + 512], lin[:, lo : lo + 512], eff_sb[hf][:, i, lo : lo + 512], MULT)
+            for lo in range(0, HALF, 256):
+                nc.gpsimd.tensor_tensor(gated[hf][:, i, lo : lo + 256], lin[:, lo : lo + 256], eff_sb[hf][:, i, lo : lo + 256], MULT)
 
         def gate_on_vector(bank, hf, i):
             nc.vector.tensor_tensor(gated[hf][:, i, :], bank[:], eff_sb[hf][:, i, :], MULT)
@@ -355,35 +355,35 @@ def tile_list_photon_triple_coincidence_kernel(
         round_w4_part(1, round_on_scalar)
         make_h(0)
         store_h(0, 256)
-        round_h(0, round_on_scalar)
+        single(0, 0, gate_on_gpsimd)
         make_h(1)
         store_h(256, 512)
-        round_h(1, round_on_scalar)
+        single(0, 1, gate_on_gpsimd)
+        single(0, 2, gate_on_gpsimd)
+        round_h(0, round_on_scalar)
         quantize_w4_part(0)
         quantize_w4_part(1)
-        single(0, 0, gate_on_vector)
-        quantize_h(0)
-        single(0, 1, gate_on_vector)
-        single(0, 2, gate_on_vector)
-        quantize_h(1)
-        store_codes(0)
         make_h(2)
         store_h(512, 768)
-        round_h(2, round_on_scalar)
+        round_h(1, round_on_scalar)
+        quantize_h(0)
+        single(1, 0, gate_on_gpsimd)
+        single(1, 1, gate_on_gpsimd)
         finish(0, False)
         store_y(0, 256)
+        quantize_h(1)
+        store_codes(0)
         make_h(3)
         store_h(768, 1024)
-        round_h(3, round_on_scalar)
+        round_h(2, round_on_scalar)
         finish(1, False)
         store_y(256, 512)
+        round_h(3, round_on_scalar)
         quantize_h(2)
-        single(1, 0, gate_on_vector)
-        single(1, 1, gate_on_vector)
         single(1, 2, gate_on_vector)
+        finish(2, False)
+        store_y(512, 768)
         quantize_h(3)
         store_codes(1)
         store_scales()
-        finish(2, False)
-        store_y(512, 768)
         finish(3, True)

@@ -18,13 +18,20 @@ ADD = mybir.AluOpType.add
 
 P = 128
 PACK = 4
-PASSES = K // (P * PACK)
+K_PASS = P * PACK
+PASSES = K // K_PASS
+QUADRANTS, QUADRANT = 4, 32
+ROWS = 4
 HALF = 512
-BANK = 512
+CHUNK = 256
+CHUNKS = S // CHUNK
 NT = N // P
-D3_PLACE = {(0, 0): "piece00", (0, 1): "piece01", (1, 0): "piece10", (1, 1): "piece11"}
-D23_PLACE = {(0, 0): "d23_00", (0, 1): "d23_01", (1, 0): "d23_10", (1, 1): "d23_11"}
-CHUNKS = ((0, 256), (256, 256), (512, 256), (768, 256))
+PIECE = H // 2
+LINE = 16
+SHIFTED = 112
+GATE_PIECE = 256
+W4_PARTS = ((0, 256), (256, N))
+ALIGN = 256
 
 
 def tile_list_photon_triple_coincidence_kernel(
@@ -38,41 +45,40 @@ def tile_list_photon_triple_coincidence_kernel(
         psum = ctx.enter_context(tc.psum_pool(name="psum", bufs=8))
 
         def held(name, shape, dtype):
-            return keep.tile(shape, dtype, name=name, align_bytes=256)
+            return keep.tile(shape, dtype, name=name, align_bytes=ALIGN)
 
-        def shared(name, tag, shape):
-            return keep.tile(shape, F32, name=name, tag=tag, align_bytes=256)
+        def shared(name, tag, shape, dtype):
+            return keep.tile(shape, dtype, name=name, tag=tag, align_bytes=ALIGN)
 
         offsets = keep.tile([P, S // 16], U16, name="offsets")
         tab_s = held("tab_s", [P, T], U8)
         tab_w = [held("tab_w%d" % a, [P, T], U32) for a in range(PASSES)]
-        w2_s_raw = keep.tile([P, PASSES * H], U8, name="w2_s_raw", tag="picked11", align_bytes=256)
-        w3_s_raw = keep.tile([P, H], U8, name="w3_s_raw", tag="picked01", align_bytes=256)
+        w2_s_raw = shared("w2_s_raw", "picked11", [P, PASSES * H], U8)
+        w3_s_raw = shared("w3_s_raw", "picked01", [P, H], U8)
         w5_s = held("w5_s", [P, PASSES * N], U8)
         v_s1 = held("v_s1", [P, S], U8)
         w3_raw = held("w3_raw", [P, PASSES * H], I32)
-        w2_raw = keep.tile([P, PASSES * H * 2], U8, name="w2_raw", tag="early", align_bytes=256)
-        v_s0 = keep.tile([P, S], U8, name="v_s0", tag="early", align_bytes=256)
+        w2_raw = shared("w2_raw", "early", [P, PASSES * H * 2], U8)
+        v_s0 = shared("v_s0", "early", [P, S], U8)
         w5_w = held("w5_w", [P, PASSES * N * 2], U8)
 
         for plane in (tab_s, w3_s_raw, w2_s_raw, v_s1, w5_s):
             nc.vector.memset(plane[:].bitcast(I32), 0)
 
         def load_planes_side_by_side(tile, scales):
-            for q in range(4):
+            for q in range(QUADRANTS):
                 nc.sync.dma_start(
-                    tile[32 * q : 32 * q + 4, :].bitcast(I32).rearrange("r (a c) -> r a c", a=PASSES),
-                    scales[:, 4 * q : 4 * q + 4, :].rearrange("a r c -> r a c").bitcast(I32))
+                    tile[QUADRANT * q : QUADRANT * q + ROWS, :].bitcast(I32).rearrange("r (a c) -> r a c", a=PASSES),
+                    scales[:, ROWS * q : ROWS * (q + 1), :].rearrange("a r c -> r a c").bitcast(I32))
 
         def load_planes_stacked(tile, scales):
-            for q in range(4):
-                nc.sync.dma_start(tile[32 * q : 32 * q + 8, :].bitcast(I32), scales[:, 4 * q : 4 * q + 4, :].bitcast(I32))
+            for q in range(QUADRANTS):
+                nc.sync.dma_start(
+                    tile[QUADRANT * q : QUADRANT * q + PASSES * ROWS, :].bitcast(I32),
+                    scales[:, ROWS * q : ROWS * (q + 1), :].bitcast(I32))
 
         def load_words(tile, words):
             nc.sync.dma_start(tile[:].bitcast(I32).rearrange("p (a c) -> p a c", a=PASSES), words.bitcast(I32))
-
-        def load_words_pass(tile, words, a):
-            nc.sync.dma_start(tile[:, a * H : (a + 1) * H], words[a].rearrange("p c i -> p (c i)").bitcast(I32))
 
         def load_table(a):
             nc.sync.dma_start(tab_w[a][:].bitcast(I32), tab_words[a].rearrange("p t i -> p (t i)").bitcast(I32))
@@ -80,15 +86,11 @@ def tile_list_photon_triple_coincidence_kernel(
         w1_raw = {}
 
         def load_w1(a, b):
-            rows = w1[a * 512 : (a + 1) * 512, :].rearrange("(p j) c -> p j c", j=PACK)
-            w1_raw[a, b] = shared("w1_raw%d%d" % (a, b), "piece%d%d" % (a, b), [P, PACK, H // 2])
-            nc.sync.dma_start(w1_raw[a, b][:], rows[:, :, b * 256 : (b + 1) * 256])
+            rows = w1[a * K_PASS : (a + 1) * K_PASS, :].rearrange("(p j) c -> p j c", j=PACK)
+            w1_raw[a, b] = shared("w1_raw%d%d" % (a, b), "piece%d%d" % (a, b), [P, PACK, PIECE], F32)
+            nc.sync.dma_start(w1_raw[a, b][:], rows[:, :, b * PIECE : (b + 1) * PIECE])
 
         eff_sb = [held("eff%d" % hf, [P, NT, HALF], F32) for hf in range(2)]
-
-        def load_eff(hf):
-            nc.sync.dma_start(eff_sb[hf][:], eff[:, hf * HALF : (hf + 1) * HALF].rearrange("(i p) j -> p i j", p=P))
-
         w4_raw = held("w4_raw", [P, PACK, N], F32)
 
         load_words(w3_raw, w3_words.rearrange("a p c i -> p a (c i)"))
@@ -99,15 +101,14 @@ def tile_list_photon_triple_coincidence_kernel(
         load_planes_stacked(w3_s_raw, w3_scales)
         load_table(1)
         load_planes_side_by_side(w2_s_raw, w2_scales)
-        load_w1(0, 0)
-        load_w1(0, 1)
-        load_w1(1, 0)
-        load_w1(1, 1)
+        for a in range(PASSES):
+            for b in range(2):
+                load_w1(a, b)
         load_words(w5_w, w5_words.rearrange("a p c -> p a c"))
         load_planes_side_by_side(w5_s, w5_scales)
         nc.sync.dma_start(w4_raw[:], w4.rearrange("(p j) n -> p j n", j=PACK))
-        load_eff(0)
-        load_eff(1)
+        for hf in range(2):
+            nc.sync.dma_start(eff_sb[hf][:], eff[:, hf * HALF : (hf + 1) * HALF].rearrange("(i p) j -> p i j", p=P))
 
         v_s = [v_s0, v_s1]
         v_w = {}
@@ -116,114 +117,90 @@ def tile_list_photon_triple_coincidence_kernel(
         w3_s = held("w3_s", [P, PACK * P], U8)
         w2_s = held("w2_s", [P, PACK * PASSES * P], U8)
 
-        def deal(dst, src, run):
+        def deal(dst, src, size):
+            run = LINE // size
             nc.vector.tensor_copy(
                 dst.rearrange("p (t g i) -> p g t i", t=PACK, i=run),
                 src.rearrange("p (g i t) -> p g t i", t=PACK, i=run))
 
-        def gather(a, hf):
-            v_w[a, hf] = keep.tile([P, HALF], U32, name="v_w%d%d" % (a, hf), tag="picked%d%d" % (a, hf), align_bytes=256)
-            nc.vector.tensor_copy(v_w[a, hf][:], tab_w[a][:].indirect(offsets[:, hf * 32 : (hf + 1) * 32]))
-
-        def gather_scales():
-            nc.vector.tensor_copy(v_s0[:], tab_s[:].indirect(offsets[:]))
-            nc.scalar.dma_start(v_s1[0:112, :].bitcast(I32), v_s0[4:116, :].bitcast(I32))
+        def gather_words(a, hf):
+            v_w[a, hf] = shared("v_w%d%d" % (a, hf), "picked%d%d" % (a, hf), [P, HALF], U32)
+            entries = offsets[:, hf * HALF // 16 : (hf + 1) * HALF // 16]
+            nc.vector.tensor_copy(v_w[a, hf][:], tab_w[a][:].indirect(entries))
 
         deal(w3_w[:], w3_raw[:], 4)
-        deal(w2_w[:].bitcast(U16), w2_raw[:].bitcast(U16), 8)
-        gather_scales()
-        gather(0, 0)
-        deal(w3_s[:], w3_s_raw[:], 16)
-        gather(0, 1)
-        gather(1, 0)
-        deal(w2_s[:], w2_s_raw[:], 16)
-        gather(1, 1)
+        deal(w2_w[:].bitcast(U16), w2_raw[:].bitcast(U16), 2)
+        nc.vector.tensor_copy(v_s0[:], tab_s[:].indirect(offsets[:]))
+        nc.scalar.dma_start(v_s1[0:SHIFTED, :].bitcast(I32), v_s0[ROWS : ROWS + SHIFTED, :].bitcast(I32))
+        for a, dealt, raw in ((0, w3_s, w3_s_raw), (1, w2_s, w2_s_raw)):
+            gather_words(a, 0)
+            deal(dealt[:], raw[:], 1)
+            gather_words(a, 1)
 
-        def cols(t, a, width):
+        def dealt_cols(t, a, width):
             return slice((t * PASSES + a) * width, (t * PASSES + a + 1) * width)
 
         w1_b = [held("w1_b%d" % a, [P, PACK * H], BF16) for a in range(PASSES)]
         w1_w = [held("w1_w%d" % a, [P, H], U32) for a in range(PASSES)]
         w1_s = [held("w1_s%d" % a, [P, H], U8) for a in range(PASSES)]
 
-        def round_on_scalar(dst, src):
-            nc.scalar.copy(dst, src)
-
-        def round_on_vector(dst, src):
-            nc.vector.tensor_copy(dst, src)
-
-        def round_on_gpsimd(dst, src):
-            nc.gpsimd.tensor_scalar(dst, src, 1.0, 0.0, MULT, ADD)
-
-        def round_w1(a, b, how):
-            how(
-                w1_b[a][:].rearrange("p (t m j) -> p m t j", t=PACK, j=PACK)[:, b * 64 : (b + 1) * 64],
-                w1_raw[a, b][:].rearrange("p j (m t) -> p m t j", t=PACK))
-
         def quantize_w1(a):
+            for b, round_copy in enumerate((nc.scalar.copy, nc.vector.tensor_copy)):
+                places = slice(b * PIECE // PACK, (b + 1) * PIECE // PACK)
+                round_copy(
+                    w1_b[a][:].rearrange("p (t m j) -> p m t j", t=PACK, j=PACK)[:, places],
+                    w1_raw[a, b][:].rearrange("p j (m t) -> p m t j", t=PACK))
             nc.vector.quantize_mx(out=w1_w[a][:].bitcast(FP8X4), scales=w1_s[a][:], in_=w1_b[a][:])
 
-        d23 = {}
+        d3_banks, d3, d23 = {}, {}, {}
 
-        def pass_w2(bank, t, a, hf):
-            nc.tensor.matmul_mx(
-                out=bank[:], lhsT=w2_w[:, cols(t, a, 2 * P)].bitcast(FP4X4), lhsT_scale=w2_s[:, cols(t, a, P)],
-                rhs=v_w[a, hf][:].bitcast(FP8X4), rhs_scale=v_s[a][:, hf * HALF : (hf + 1) * HALF],
-                start=(a == 0), stop=(a == PASSES - 1))
-
-        def pass_w3(bank, t, a, hf):
-            nc.tensor.matmul_mx(
-                out=bank[:], lhsT=w3_w[:, cols(t, a, P)].bitcast(FP8X4),
-                lhsT_scale=w3_s[4 * a : P, t * P : (t + 1) * P],
-                rhs=v_w[a, hf][:].bitcast(FP8X4), rhs_scale=v_s0[4 * a : P, hf * HALF : (hf + 1) * HALF],
-                start=(a == 0), stop=(a == PASSES - 1))
-
-        banks_3 = {}
-        d3 = {}
-
-        def products_3(hf, a):
+        def w3_pass(hf, a):
             for t in range(PACK):
                 if a == 0:
-                    banks_3[t, hf] = psum.tile([P, HALF], F32, name="bank")
-                pass_w3(banks_3[t, hf], t, a, hf)
+                    d3_banks[t, hf] = psum.tile([P, HALF], F32, name="bank")
+                nc.tensor.matmul_mx(
+                    out=d3_banks[t, hf][:], lhsT=w3_w[:, dealt_cols(t, a, P)].bitcast(FP8X4),
+                    lhsT_scale=w3_s[ROWS * a : P, t * P : (t + 1) * P],
+                    rhs=v_w[a, hf][:].bitcast(FP8X4), rhs_scale=v_s0[ROWS * a : P, hf * HALF : (hf + 1) * HALF],
+                    start=(a == 0), stop=(a == PASSES - 1))
 
-        def copy_3(t, hf):
+        def copy_d3(t, hf):
             if t % 2 == 0:
-                d3[hf, t // 2] = shared("d3_%d%d" % (hf, t // 2), D3_PLACE[hf, t // 2], [P, 2, HALF])
-            nc.scalar.copy(d3[hf, t // 2][:, t % 2, :], banks_3[t, hf][:])
+                d3[hf, t // 2] = shared("d3_%d%d" % (hf, t // 2), "piece%d%d" % (hf, t // 2), [P, 2, HALF], F32)
+            nc.scalar.copy(d3[hf, t // 2][:, t % 2, :], d3_banks[t, hf][:])
 
-        def product_2(t, hf):
+        def make_d23(t, hf):
             bank = psum.tile([P, HALF], F32, name="bank")
             for a in range(PASSES):
-                pass_w2(bank, t, a, hf)
+                nc.tensor.matmul_mx(
+                    out=bank[:], lhsT=w2_w[:, dealt_cols(t, a, 2 * P)].bitcast(FP4X4),
+                    lhsT_scale=w2_s[:, dealt_cols(t, a, P)],
+                    rhs=v_w[a, hf][:].bitcast(FP8X4), rhs_scale=v_s[a][:, hf * HALF : (hf + 1) * HALF],
+                    start=(a == 0), stop=(a == PASSES - 1))
             if t % 2 == 0:
-                d23[hf, t // 2] = shared("d23_%d%d" % (hf, t // 2), D23_PLACE[hf, t // 2], [P, 2, HALF])
+                d23[hf, t // 2] = held("d23_%d%d" % (hf, t // 2), [P, 2, HALF], F32)
             nc.vector.tensor_tensor(d23[hf, t // 2][:, t % 2, :], bank[:], d3[hf, t // 2][:, t % 2, :], MULT)
+
+        def copy_d3_then_make_d23(slices, hf):
+            for t in slices:
+                copy_d3(t, hf)
+            for t in slices:
+                make_d23(t, hf)
 
         w4_b = held("w4_b", [P, N * PACK], BF16)
         w4_w = held("w4_w", [P, N], U32)
         w4_s = held("w4_s", [P, N], U8)
 
-        def round_w4(how):
-            how(
-                w4_b[:].rearrange("p (c i j) -> p c j i", i=4, j=PACK),
-                w4_raw[:].rearrange("p j (c i) -> p c j i", i=4))
-
-        W4_PARTS = ((0, 256), (256, N))
-
-        def round_w4_part(k, how):
-            lo, hi = W4_PARTS[k]
-            how(
-                w4_b[:, PACK * lo : PACK * hi].rearrange("p (c i j) -> p c j i", i=4, j=PACK),
-                w4_raw[:, :, lo:hi].rearrange("p j (c i) -> p c j i", i=4))
-
-        def quantize_w4_part(k):
-            lo, hi = W4_PARTS[k]
-            nc.vector.quantize_mx(out=w4_w[:, lo:hi].bitcast(FP8X4), scales=w4_s[:, lo:hi], in_=w4_b[:, PACK * lo : PACK * hi])
+        def round_w4():
+            for lo, hi in W4_PARTS:
+                nc.scalar.copy(
+                    w4_b[:, PACK * lo : PACK * hi].rearrange("p (c i j) -> p c j i", i=LINE // 4, j=PACK),
+                    w4_raw[:, :, lo:hi].rearrange("p j (c i) -> p c j i", i=LINE // 4))
 
         def quantize_w4():
-            for lo, hi in ((0, 256), (256, N)):
-                nc.vector.quantize_mx(out=w4_w[:, lo:hi].bitcast(FP8X4), scales=w4_s[:, lo:hi], in_=w4_b[:, PACK * lo : PACK * hi])
+            for lo, hi in W4_PARTS:
+                nc.vector.quantize_mx(
+                    out=w4_w[:, lo:hi].bitcast(FP8X4), scales=w4_s[:, lo:hi], in_=w4_b[:, PACK * lo : PACK * hi])
 
         h_w = [held("h_w%d" % hf, [P, HALF], U32) for hf in range(2)]
         h_s = held("h_s", [P, S], U8)
@@ -232,158 +209,122 @@ def tile_list_photon_triple_coincidence_kernel(
         h = [held("h%d" % hf, [P, PACK, HALF], F32) for hf in range(2)]
         y = [held("y%d" % hf, [P, NT, HALF], F32) for hf in range(2)]
 
-        def gate_on_gpsimd(bank, hf, i):
-            lin = ring.tile([P, HALF], F32, name="lin", bufs=6)
-            nc.scalar.copy(lin[:], bank[:])
-            for lo in range(0, HALF, 256):
-                nc.gpsimd.tensor_tensor(gated[hf][:, i, lo : lo + 256], lin[:, lo : lo + 256], eff_sb[hf][:, i, lo : lo + 256], MULT)
+        def chunk(c):
+            hf, lo = divmod(c * CHUNK, HALF)
+            return hf, slice(lo, lo + CHUNK), slice(c * CHUNK, (c + 1) * CHUNK)
 
-        def gate_on_vector(bank, hf, i):
-            nc.vector.tensor_tensor(gated[hf][:, i, :], bank[:], eff_sb[hf][:, i, :], MULT)
-
-        def single(hf, i, gate):
-            hcols = slice(hf * HALF, (hf + 1) * HALF)
+        def w5_product(hf, i):
             bank = psum.tile([P, HALF], F32, name="bank")
             for a in range(PASSES):
+                first = a * N + i * P
                 nc.tensor.matmul_mx(
-                    out=bank[:],
-                    lhsT=w5_w[:, 2 * (a * N + i * P) : 2 * (a * N + (i + 1) * P)].bitcast(FP4X4),
-                    lhsT_scale=w5_s[:, a * N + i * P : a * N + (i + 1) * P],
-                    rhs=v_w[a, hf][:].bitcast(FP8X4), rhs_scale=v_s[a][:, hcols],
+                    out=bank[:], lhsT=w5_w[:, 2 * first : 2 * (first + P)].bitcast(FP4X4),
+                    lhsT_scale=w5_s[:, first : first + P],
+                    rhs=v_w[a, hf][:].bitcast(FP8X4), rhs_scale=v_s[a][:, hf * HALF : (hf + 1) * HALF],
                     start=(a == 0), stop=(a == PASSES - 1))
-            gate(bank, hf, i)
+            return bank
+
+        def gate_on_gpsimd(hf, i):
+            bank = w5_product(hf, i)
+            lin = ring.tile([P, HALF], F32, name="lin", bufs=2 * NT)
+            nc.scalar.copy(lin[:], bank[:])
+            for lo in range(0, HALF, GATE_PIECE):
+                cols = slice(lo, lo + GATE_PIECE)
+                nc.gpsimd.tensor_tensor(gated[hf][:, i, cols], lin[:, cols], eff_sb[hf][:, i, cols], MULT)
+
+        def gate_on_vector(hf, i):
+            bank = w5_product(hf, i)
+            nc.vector.tensor_tensor(gated[hf][:, i, :], bank[:], eff_sb[hf][:, i, :], MULT)
 
         def make_h(c):
-            j0, width = CHUNKS[c]
-            hf, lo = j0 // HALF, j0 % HALF
-            per_bank = BANK // width
-            for t0 in range(0, PACK, per_bank):
-                bank = psum.tile([P, per_bank, width], F32, name="bank")
-                for e in range(per_bank):
-                    t = t0 + e
+            hf, in_half, in_list = chunk(c)
+            for pair in range(PACK // 2):
+                bank = psum.tile([P, 2, CHUNK], F32, name="bank")
+                for e in range(2):
+                    t = 2 * pair + e
                     for a in range(PASSES):
                         nc.tensor.matmul_mx(
                             out=bank[:, e, :], lhsT=w1_w[a][:, t * P : (t + 1) * P].bitcast(FP8X4),
                             lhsT_scale=w1_s[a][:, t * P : (t + 1) * P],
-                            rhs=v_w[a, hf][:, lo : lo + width].bitcast(FP8X4),
-                            rhs_scale=v_s[a][:, j0 : j0 + width],
+                            rhs=v_w[a, hf][:, in_half].bitcast(FP8X4), rhs_scale=v_s[a][:, in_list],
                             start=(a == 0), stop=(a == PASSES - 1))
                 nc.vector.tensor_tensor(
-                    h[hf][:, t0 : t0 + per_bank, lo : lo + width], bank[:],
-                    d23[hf, t0 // 2][:, :, lo : lo + width], MULT)
+                    h[hf][:, 2 * pair : 2 * pair + 2, in_half], bank[:], d23[hf, pair][:, :, in_half], MULT)
+            nc.sync.dma_start(out_1[:, in_list].rearrange("(p t) j -> p t j", t=PACK), h[hf][:, :, in_half])
 
-        def round_h(c, how):
-            j0, width = CHUNKS[c]
-            hf, lo = j0 // HALF, j0 % HALF
-            h_b[c] = held("h_b%d" % c, [P, width * PACK], BF16)
-            how(
-                h_b[c][:].rearrange("p (c i t) -> p c t i", i=4, t=PACK),
-                h[hf][:, :, lo : lo + width].rearrange("p t (c i) -> p c t i", i=4))
-
-        def store_h(j0, j1):
-            hf = j0 // HALF
-            nc.sync.dma_start(
-                out_1[:, j0:j1].rearrange("(p t) j -> p t j", t=PACK), h[hf][:, :, j0 - hf * HALF : j1 - hf * HALF])
-
-        def store_y(j0, j1):
-            hf = j0 // HALF
-            nc.sync.dma_start(
-                out_0[:, j0:j1].rearrange("(i p) j -> p i j", p=P), y[hf][:, :, j0 - hf * HALF : j1 - hf * HALF])
+        def round_h(c):
+            hf, in_half = chunk(c)[:2]
+            h_b[c] = held("h_b%d" % c, [P, CHUNK * PACK], BF16)
+            nc.scalar.copy(
+                h_b[c][:].rearrange("p (c i t) -> p c t i", i=LINE // 4, t=PACK),
+                h[hf][:, :, in_half].rearrange("p t (c i) -> p c t i", i=LINE // 4))
 
         def quantize_h(c):
-            j0, width = CHUNKS[c]
-            hf, lo = j0 // HALF, j0 % HALF
-            nc.vector.quantize_mx(
-                out=h_w[hf][:, lo : lo + width].bitcast(FP8X4), scales=h_s[:, j0 : j0 + width], in_=h_b[c][:])
+            hf, in_half, in_list = chunk(c)
+            nc.vector.quantize_mx(out=h_w[hf][:, in_half].bitcast(FP8X4), scales=h_s[:, in_list], in_=h_b[c][:])
+            if in_half.stop == HALF:
+                nc.sync.dma_start(
+                    out_2[0, :, hf * HALF : (hf + 1) * HALF, :].rearrange("p m t -> p (m t)").bitcast(I32),
+                    h_w[hf][:].bitcast(I32))
+            if in_list.stop == S:
+                for q in range(QUADRANTS):
+                    nc.scalar.dma_start(
+                        out_3[0, ROWS * q : ROWS * (q + 1), :].bitcast(I32),
+                        h_s[QUADRANT * q : QUADRANT * q + ROWS, :].bitcast(I32))
 
-        def store_codes(hf):
+        def store_y(c, i0, i1):
+            hf, in_half, in_list = chunk(c)
             nc.sync.dma_start(
-                out_2[0, :, hf * HALF : (hf + 1) * HALF, :].rearrange("p m t -> p (m t)").bitcast(I32),
-                h_w[hf][:].bitcast(I32))
+                out_0[i0 * P : i1 * P, in_list].rearrange("(i p) j -> p i j", p=P), y[hf][:, i0:i1, in_half])
 
-        def store_scales():
-            for q in range(4):
-                nc.scalar.dma_start(out_3[0, 4 * q : 4 * q + 4, :].bitcast(I32), h_s[32 * q : 32 * q + 4, :].bitcast(I32))
-
-        def finish(c, store_each):
-            j0, width = CHUNKS[c]
-            hf, lo = j0 // HALF, j0 % HALF
-            per_bank = BANK // width
-            for i0 in range(0, NT, per_bank):
-                i1 = min(i0 + per_bank, NT)
-                bank = psum.tile([P, per_bank, width], F32, name="bank")
+        def make_y(c):
+            hf, in_half, in_list = chunk(c)
+            last = c == CHUNKS - 1
+            for i0 in range(0, NT, 2):
+                i1 = min(i0 + 2, NT)
+                bank = psum.tile([P, 2, CHUNK], F32, name="bank")
                 for i in range(i0, i1):
                     nc.tensor.matmul_mx(
                         out=bank[:, i - i0, :], lhsT=w4_w[:, i * P : (i + 1) * P].bitcast(FP8X4),
                         lhsT_scale=w4_s[:, i * P : (i + 1) * P],
-                        rhs=h_w[hf][:, lo : lo + width].bitcast(FP8X4),
-                        rhs_scale=h_s[:, j0 : j0 + width], start=True, stop=True)
+                        rhs=h_w[hf][:, in_half].bitcast(FP8X4), rhs_scale=h_s[:, in_list], start=True, stop=True)
                 nc.vector.tensor_tensor(
-                    y[hf][:, i0:i1, lo : lo + width], bank[:, 0 : i1 - i0, :], gated[hf][:, i0:i1, lo : lo + width], ADD)
-                if store_each:
-                    nc.sync.dma_start(
-                        out_0[i0 * P : i1 * P, j0 : j0 + width].rearrange("(i p) j -> p i j", p=P),
-                        y[hf][:, i0:i1, lo : lo + width])
+                    y[hf][:, i0:i1, in_half], bank[:, 0 : i1 - i0, :], gated[hf][:, i0:i1, in_half], ADD)
+                if last:
+                    store_y(c, i0, i1)
+            if not last:
+                store_y(c, 0, NT)
 
-        products_3(0, 0)
-        products_3(1, 0)
-        products_3(0, 1)
-        round_w1(0, 0, round_on_scalar)
-        round_w1(0, 1, round_on_vector)
+        w3_pass(0, 0)
+        w3_pass(1, 0)
+        w3_pass(0, 1)
         quantize_w1(0)
-        copy_3(0, 0)
-        copy_3(1, 0)
-        product_2(0, 0)
-        product_2(1, 0)
-        products_3(1, 1)
-        copy_3(2, 0)
-        copy_3(3, 0)
-        product_2(2, 0)
-        product_2(3, 0)
-        round_w1(1, 0, round_on_scalar)
-        round_w1(1, 1, round_on_vector)
+        copy_d3_then_make_d23((0, 1), 0)
+        w3_pass(1, 1)
+        copy_d3_then_make_d23((2, 3), 0)
         quantize_w1(1)
-        copy_3(0, 1)
-        copy_3(1, 1)
-        copy_3(2, 1)
-        copy_3(3, 1)
-        product_2(0, 1)
-        product_2(1, 1)
-        product_2(2, 1)
-        product_2(3, 1)
-        round_w4_part(0, round_on_scalar)
-        round_w4_part(1, round_on_scalar)
+        copy_d3_then_make_d23(range(PACK), 1)
+        round_w4()
+        quantize_w4()
         make_h(0)
-        store_h(0, 256)
-        single(0, 0, gate_on_gpsimd)
+        gate_on_gpsimd(0, 0)
         make_h(1)
-        store_h(256, 512)
-        single(0, 1, gate_on_gpsimd)
-        single(0, 2, gate_on_gpsimd)
-        round_h(0, round_on_scalar)
-        quantize_w4_part(0)
-        quantize_w4_part(1)
+        gate_on_gpsimd(0, 1)
+        gate_on_gpsimd(0, 2)
+        round_h(0)
         make_h(2)
-        store_h(512, 768)
-        round_h(1, round_on_scalar)
+        round_h(1)
         quantize_h(0)
-        single(1, 0, gate_on_gpsimd)
-        single(1, 1, gate_on_gpsimd)
-        finish(0, False)
-        store_y(0, 256)
+        gate_on_gpsimd(1, 0)
+        gate_on_gpsimd(1, 1)
+        make_y(0)
         quantize_h(1)
-        store_codes(0)
         make_h(3)
-        store_h(768, 1024)
-        round_h(2, round_on_scalar)
-        finish(1, False)
-        store_y(256, 512)
-        round_h(3, round_on_scalar)
+        round_h(2)
+        make_y(1)
+        round_h(3)
         quantize_h(2)
-        single(1, 2, gate_on_vector)
-        finish(2, False)
-        store_y(512, 768)
+        gate_on_vector(1, 2)
+        make_y(2)
         quantize_h(3)
-        store_codes(1)
-        store_scales()
-        finish(3, True)
+        make_y(3)

@@ -31,6 +31,7 @@ LINE = 16
 SHIFTED = 112
 GATE_PIECE = 256
 W4_PARTS = ((0, 256), (256, N))
+BANKS = 8
 ALIGN = 256
 
 
@@ -42,7 +43,7 @@ def tile_list_photon_triple_coincidence_kernel(
     with ExitStack() as ctx:
         keep = ctx.enter_context(tc.tile_pool(name="keep", bufs=1))
         ring = ctx.enter_context(tc.tile_pool(name="ring", bufs=3))
-        psum = ctx.enter_context(tc.psum_pool(name="psum", bufs=8))
+        psum = ctx.enter_context(tc.psum_pool(name="psum", bufs=BANKS))
 
         def held(name, shape, dtype):
             return keep.tile(shape, dtype, name=name, align_bytes=ALIGN)
@@ -50,20 +51,28 @@ def tile_list_photon_triple_coincidence_kernel(
         def shared(name, tag, shape, dtype):
             return keep.tile(shape, dtype, name=name, tag=tag, align_bytes=ALIGN)
 
+        banks_used = []
+
+        def next_bank(shape):
+            number = len(banks_used)
+            banks_used.append(number)
+            return psum.tile(shape, F32, name="sum%d" % number, tag="bank")
+
         offsets = keep.tile([P, S // 16], U16, name="offsets")
         tab_s = held("tab_s", [P, T], U8)
         tab_w = [held("tab_w%d" % a, [P, T], U32) for a in range(PASSES)]
-        w2_s_raw = shared("w2_s_raw", "picked11", [P, PASSES * H], U8)
+        w2_s_raw = held("w2_s_raw", [P, PASSES * H], U8)
         w3_s_raw = shared("w3_s_raw", "picked01", [P, H], U8)
         w5_s = held("w5_s", [P, PASSES * N], U8)
         v_s1 = held("v_s1", [P, S], U8)
         w3_raw = held("w3_raw", [P, PASSES * H], I32)
-        w2_raw = shared("w2_raw", "early", [P, PASSES * H * 2], U8)
-        v_s0 = shared("v_s0", "early", [P, S], U8)
+        w2_raw = held("w2_raw", [P, PASSES * H * 2], U8)
+        v_s0 = held("v_s0", [P, S], U8)
         w5_w = held("w5_w", [P, PASSES * N * 2], U8)
 
         for plane in (tab_s, w3_s_raw, w2_s_raw, v_s1, w5_s):
             nc.vector.memset(plane[:].bitcast(I32), 0)
+
 
         def load_planes_side_by_side(tile, scales):
             for q in range(QUADRANTS):
@@ -93,29 +102,8 @@ def tile_list_photon_triple_coincidence_kernel(
         eff_sb = [held("eff%d" % hf, [P, NT, HALF], F32) for hf in range(2)]
         w4_raw = held("w4_raw", [P, PACK, N], F32)
 
-        load_words(w3_raw, w3_words.rearrange("a p c i -> p a (c i)"))
-        load_words(w2_raw, w2_words.rearrange("a p c -> p a c"))
-        nc.sync.dma_start(offsets[:], offs)
-        load_planes_stacked(tab_s, tab_scales)
-        load_table(0)
-        load_planes_stacked(w3_s_raw, w3_scales)
-        load_table(1)
-        load_planes_side_by_side(w2_s_raw, w2_scales)
-        for a in range(PASSES):
-            for b in range(2):
-                load_w1(a, b)
-        load_words(w5_w, w5_words.rearrange("a p c -> p a c"))
-        load_planes_side_by_side(w5_s, w5_scales)
-        nc.sync.dma_start(w4_raw[:], w4.rearrange("(p j) n -> p j n", j=PACK))
-        for hf in range(2):
+        def load_eff(hf):
             nc.sync.dma_start(eff_sb[hf][:], eff[:, hf * HALF : (hf + 1) * HALF].rearrange("(i p) j -> p i j", p=P))
-
-        v_s = [v_s0, v_s1]
-        v_w = {}
-        w3_w = held("w3_w", [P, PACK * PASSES * P], I32)
-        w2_w = held("w2_w", [P, PACK * PASSES * P * 2], U8)
-        w3_s = held("w3_s", [P, PACK * P], U8)
-        w2_s = held("w2_s", [P, PACK * PASSES * P], U8)
 
         def deal(dst, src, size):
             run = LINE // size
@@ -123,19 +111,47 @@ def tile_list_photon_triple_coincidence_kernel(
                 dst.rearrange("p (t g i) -> p g t i", t=PACK, i=run),
                 src.rearrange("p (g i t) -> p g t i", t=PACK, i=run))
 
+        w2_w = held("w2_w", [P, PACK * PASSES * P * 2], U8)
+
+        nc.sync.dma_start(offsets[:], offs)
+        load_words(w2_raw, w2_words.rearrange("a p c -> p a c"))
+        load_planes_stacked(tab_s, tab_scales)
+        load_table(0)
+        load_words(w3_raw, w3_words.rearrange("a p c i -> p a (c i)"))
+        load_planes_stacked(w3_s_raw, w3_scales)
+        load_table(1)
+        load_w1(0, 0)
+        load_planes_side_by_side(w2_s_raw, w2_scales)
+        deal(w2_w[:].bitcast(U16), w2_raw[:].bitcast(U16), 2)
+        nc.vector.tensor_copy(v_s0[:], tab_s[:].indirect(offsets[:]))
+        nc.sync.dma_start(v_s1[0:SHIFTED, :].bitcast(I32), v_s0[ROWS : ROWS + SHIFTED, :].bitcast(I32))
+        load_w1(0, 1)
+        load_w1(1, 0)
+        load_w1(1, 1)
+        load_words(w5_w, w5_words.rearrange("a p c -> p a c"))
+        load_planes_side_by_side(w5_s, w5_scales)
+        nc.sync.dma_start(w4_raw[:], w4.rearrange("(p j) n -> p j n", j=PACK))
+        load_eff(0)
+        load_eff(1)
+
+        v_s = [v_s0, v_s1]
+        v_w = {}
+        w3_w = held("w3_w", [P, PACK * PASSES * P], I32)
+        w3_s = held("w3_s", [P, PACK * P], U8)
+        w2_s = held("w2_s", [P, PACK * PASSES * P], U8)
+
         def gather_words(a, hf):
             v_w[a, hf] = shared("v_w%d%d" % (a, hf), "picked%d%d" % (a, hf), [P, HALF], U32)
             entries = offsets[:, hf * HALF // 16 : (hf + 1) * HALF // 16]
             nc.vector.tensor_copy(v_w[a, hf][:], tab_w[a][:].indirect(entries))
 
+        gather_words(0, 0)
         deal(w3_w[:], w3_raw[:], 4)
-        deal(w2_w[:].bitcast(U16), w2_raw[:].bitcast(U16), 2)
-        nc.vector.tensor_copy(v_s0[:], tab_s[:].indirect(offsets[:]))
-        nc.scalar.dma_start(v_s1[0:SHIFTED, :].bitcast(I32), v_s0[ROWS : ROWS + SHIFTED, :].bitcast(I32))
-        for a, dealt, raw in ((0, w3_s, w3_s_raw), (1, w2_s, w2_s_raw)):
-            gather_words(a, 0)
-            deal(dealt[:], raw[:], 1)
-            gather_words(a, 1)
+        deal(w3_s[:], w3_s_raw[:], 1)
+        gather_words(0, 1)
+        gather_words(1, 0)
+        gather_words(1, 1)
+        deal(w2_s[:], w2_s_raw[:], 1)
 
         def dealt_cols(t, a, width):
             return slice((t * PASSES + a) * width, (t * PASSES + a + 1) * width)
@@ -145,11 +161,11 @@ def tile_list_photon_triple_coincidence_kernel(
         w1_s = [held("w1_s%d" % a, [P, H], U8) for a in range(PASSES)]
 
         def quantize_w1(a):
-            for b, round_copy in enumerate((nc.scalar.copy, nc.vector.tensor_copy)):
+            for b, round_copy in enumerate((nc.scalar.copy, nc.scalar.copy)):
                 places = slice(b * PIECE // PACK, (b + 1) * PIECE // PACK)
                 round_copy(
-                    w1_b[a][:].rearrange("p (t m j) -> p m t j", t=PACK, j=PACK)[:, places],
-                    w1_raw[a, b][:].rearrange("p j (m t) -> p m t j", t=PACK))
+                    w1_b[a][:].rearrange("p (t m j) -> p m j t", t=PACK, j=PACK)[:, places],
+                    w1_raw[a, b][:].rearrange("p j (m t) -> p m j t", t=PACK))
             nc.vector.quantize_mx(out=w1_w[a][:].bitcast(FP8X4), scales=w1_s[a][:], in_=w1_b[a][:])
 
         d3_banks, d3, d23 = {}, {}, {}
@@ -157,7 +173,7 @@ def tile_list_photon_triple_coincidence_kernel(
         def w3_pass(hf, a):
             for t in range(PACK):
                 if a == 0:
-                    d3_banks[t, hf] = psum.tile([P, HALF], F32, name="bank")
+                    d3_banks[t, hf] = next_bank([P, HALF])
                 nc.tensor.matmul_mx(
                     out=d3_banks[t, hf][:], lhsT=w3_w[:, dealt_cols(t, a, P)].bitcast(FP8X4),
                     lhsT_scale=w3_s[ROWS * a : P, t * P : (t + 1) * P],
@@ -165,12 +181,18 @@ def tile_list_photon_triple_coincidence_kernel(
                     start=(a == 0), stop=(a == PASSES - 1))
 
         def copy_d3(t, hf):
-            if t % 2 == 0:
-                d3[hf, t // 2] = shared("d3_%d%d" % (hf, t // 2), "piece%d%d" % (hf, t // 2), [P, 2, HALF], F32)
-            nc.scalar.copy(d3[hf, t // 2][:, t % 2, :], d3_banks[t, hf][:])
+            if (hf, t) == (0, 0):
+                whole = shared("d3_0", "piece01", [P, PACK, HALF], F32)
+                for u in range(PACK):
+                    d3[0, u] = whole[:, u, :]
+            if hf == 1 and t % 2 == 0:
+                pair = shared("d3_1%d" % (t // 2), "piece1%d" % (t // 2), [P, 2, HALF], F32)
+                for u in range(2):
+                    d3[1, t + u] = pair[:, u, :]
+            nc.scalar.copy(d3[hf, t], d3_banks[t, hf][:])
 
         def make_d23(t, hf):
-            bank = psum.tile([P, HALF], F32, name="bank")
+            bank = next_bank([P, HALF])
             for a in range(PASSES):
                 nc.tensor.matmul_mx(
                     out=bank[:], lhsT=w2_w[:, dealt_cols(t, a, 2 * P)].bitcast(FP4X4),
@@ -179,7 +201,7 @@ def tile_list_photon_triple_coincidence_kernel(
                     start=(a == 0), stop=(a == PASSES - 1))
             if t % 2 == 0:
                 d23[hf, t // 2] = held("d23_%d%d" % (hf, t // 2), [P, 2, HALF], F32)
-            nc.vector.tensor_tensor(d23[hf, t // 2][:, t % 2, :], bank[:], d3[hf, t // 2][:, t % 2, :], MULT)
+            nc.vector.tensor_tensor(d23[hf, t // 2][:, t % 2, :], bank[:], d3[hf, t], MULT)
 
         def copy_d3_then_make_d23(slices, hf):
             for t in slices:
@@ -193,9 +215,9 @@ def tile_list_photon_triple_coincidence_kernel(
 
         def round_w4():
             for lo, hi in W4_PARTS:
-                nc.scalar.copy(
-                    w4_b[:, PACK * lo : PACK * hi].rearrange("p (c i j) -> p c j i", i=LINE // 4, j=PACK),
-                    w4_raw[:, :, lo:hi].rearrange("p j (c i) -> p c j i", i=LINE // 4))
+                nc.gpsimd.tensor_scalar(
+                    w4_b[:, PACK * lo : PACK * hi].rearrange("p (c j) -> p c j", j=PACK),
+                    w4_raw[:, :, lo:hi].rearrange("p j c -> p c j"), 1.0, 0.0, MULT, ADD)
 
         def quantize_w4():
             for lo, hi in W4_PARTS:
@@ -214,7 +236,7 @@ def tile_list_photon_triple_coincidence_kernel(
             return hf, slice(lo, lo + CHUNK), slice(c * CHUNK, (c + 1) * CHUNK)
 
         def w5_product(hf, i):
-            bank = psum.tile([P, HALF], F32, name="bank")
+            bank = next_bank([P, HALF])
             for a in range(PASSES):
                 first = a * N + i * P
                 nc.tensor.matmul_mx(
@@ -239,7 +261,7 @@ def tile_list_photon_triple_coincidence_kernel(
         def make_h(c):
             hf, in_half, in_list = chunk(c)
             for pair in range(PACK // 2):
-                bank = psum.tile([P, 2, CHUNK], F32, name="bank")
+                bank = next_bank([P, 2, CHUNK])
                 for e in range(2):
                     t = 2 * pair + e
                     for a in range(PASSES):
@@ -282,7 +304,7 @@ def tile_list_photon_triple_coincidence_kernel(
             last = c == CHUNKS - 1
             for i0 in range(0, NT, 2):
                 i1 = min(i0 + 2, NT)
-                bank = psum.tile([P, 2, CHUNK], F32, name="bank")
+                bank = next_bank([P, 2, CHUNK])
                 for i in range(i0, i1):
                     nc.tensor.matmul_mx(
                         out=bank[:, i - i0, :], lhsT=w4_w[:, i * P : (i + 1) * P].bitcast(FP8X4),

@@ -215,9 +215,9 @@ def tile_list_photon_triple_coincidence_kernel(
 
         def round_w4():
             for lo, hi in W4_PARTS:
-                nc.gpsimd.tensor_scalar(
-                    w4_b[:, PACK * lo : PACK * hi].rearrange("p (c j) -> p c j", j=PACK),
-                    w4_raw[:, :, lo:hi].rearrange("p j c -> p c j"), 1.0, 0.0, MULT, ADD)
+                nc.scalar.copy(
+                    w4_b[:, PACK * lo : PACK * hi].rearrange("p (c i j) -> p c j i", i=LINE // 4, j=PACK),
+                    w4_raw[:, :, lo:hi].rearrange("p j (c i) -> p c j i", i=LINE // 4))
 
         def quantize_w4():
             for lo, hi in W4_PARTS:

@@ -126,8 +126,10 @@ def tile_list_photon_triple_coincidence_kernel(
         nc.vector.tensor_copy(v_s0[:], tab_s[:].indirect(offsets[:]))
         nc.sync.dma_start(v_s1[0:SHIFTED, :].bitcast(I32), v_s0[ROWS : ROWS + SHIFTED, :].bitcast(I32))
         load_w1(0, 1)
-        load_w1(1, 0)
-        load_w1(1, 1)
+        w1_pass1 = shared("w1_raw1", "pass1", [P, PACK, H], F32)
+        nc.sync.dma_start(w1_pass1[:], w1[K_PASS:K, :].rearrange("(p j) c -> p j c", j=PACK))
+        for b in range(2):
+            w1_raw[1, b] = w1_pass1[:, :, b * PIECE : (b + 1) * PIECE]
         load_words(w5_w, w5_words.rearrange("a p c -> p a c"))
         load_planes_side_by_side(w5_s, w5_scales)
         nc.sync.dma_start(w4_raw[:], w4.rearrange("(p j) n -> p j n", j=PACK))
@@ -160,12 +162,14 @@ def tile_list_photon_triple_coincidence_kernel(
         w1_w = [held("w1_w%d" % a, [P, H], U32) for a in range(PASSES)]
         w1_s = [held("w1_s%d" % a, [P, H], U8) for a in range(PASSES)]
 
-        def quantize_w1(a):
-            for b, round_copy in enumerate((nc.scalar.copy, nc.scalar.copy)):
+        def round_w1(a):
+            for b, round_copy in enumerate((nc.scalar.copy, nc.vector.tensor_copy if a else nc.scalar.copy)):
                 places = slice(b * PIECE // PACK, (b + 1) * PIECE // PACK)
                 round_copy(
                     w1_b[a][:].rearrange("p (t m j) -> p m j t", t=PACK, j=PACK)[:, places],
                     w1_raw[a, b][:].rearrange("p j (m t) -> p m j t", t=PACK))
+
+        def quantize_w1(a):
             nc.vector.quantize_mx(out=w1_w[a][:].bitcast(FP8X4), scales=w1_s[a][:], in_=w1_b[a][:])
 
         d3_banks, d3, d23 = {}, {}, {}
@@ -181,14 +185,10 @@ def tile_list_photon_triple_coincidence_kernel(
                     start=(a == 0), stop=(a == PASSES - 1))
 
         def copy_d3(t, hf):
-            if (hf, t) == (0, 0):
-                whole = shared("d3_0", "piece01", [P, PACK, HALF], F32)
+            if t == 0:
+                whole = shared("d3_%d" % hf, "pass1" if hf else "piece01", [P, PACK, HALF], F32)
                 for u in range(PACK):
-                    d3[0, u] = whole[:, u, :]
-            if hf == 1 and t % 2 == 0:
-                pair = shared("d3_1%d" % (t // 2), "piece1%d" % (t // 2), [P, 2, HALF], F32)
-                for u in range(2):
-                    d3[1, t + u] = pair[:, u, :]
+                    d3[hf, u] = whole[:, u, :]
             nc.scalar.copy(d3[hf, t], d3_banks[t, hf][:])
 
         def make_d23(t, hf):
@@ -200,7 +200,8 @@ def tile_list_photon_triple_coincidence_kernel(
                     rhs=v_w[a, hf][:].bitcast(FP8X4), rhs_scale=v_s[a][:, hf * HALF : (hf + 1) * HALF],
                     start=(a == 0), stop=(a == PASSES - 1))
             if t % 2 == 0:
-                d23[hf, t // 2] = held("d23_%d%d" % (hf, t // 2), [P, 2, HALF], F32)
+                name = "d23_%d%d" % (hf, t // 2)
+                d23[hf, t // 2] = held(name, [P, 2, HALF], F32)
             nc.vector.tensor_tensor(d23[hf, t // 2][:, t % 2, :], bank[:], d3[hf, t], MULT)
 
         def copy_d3_then_make_d23(slices, hf):
@@ -320,10 +321,15 @@ def tile_list_photon_triple_coincidence_kernel(
         w3_pass(0, 0)
         w3_pass(1, 0)
         w3_pass(0, 1)
+        round_w1(0)
         quantize_w1(0)
         copy_d3_then_make_d23((0, 1), 0)
         w3_pass(1, 1)
-        copy_d3_then_make_d23((2, 3), 0)
+        for t in (2, 3):
+            copy_d3(t, 0)
+        round_w1(1)
+        for t in (2, 3):
+            make_d23(t, 0)
         quantize_w1(1)
         copy_d3_then_make_d23(range(PACK), 1)
         round_w4()
@@ -347,6 +353,6 @@ def tile_list_photon_triple_coincidence_kernel(
         round_h(3)
         quantize_h(2)
         gate_on_vector(1, 2)
-        make_y(2)
         quantize_h(3)
+        make_y(2)
         make_y(3)

@@ -28,7 +28,8 @@ CHUNKS = S // CHUNK
 NT = N // P
 PIECE = H // 2
 LINE = 16
-SHIFTED = 112
+APART = 16
+SHIFTED = P - APART
 GATE_PIECE = 256
 W4_PARTS = ((0, 256), (256, N))
 BANKS = 8
@@ -86,6 +87,12 @@ def tile_list_photon_triple_coincidence_kernel(
                     tile[QUADRANT * q : QUADRANT * q + PASSES * ROWS, :].bitcast(I32),
                     scales[:, ROWS * q : ROWS * (q + 1), :].bitcast(I32))
 
+        def load_planes_apart(tile, scales):
+            for r in range(ROWS):
+                nc.sync.dma_start(
+                    tile[r:P:APART, :].bitcast(I32),
+                    scales[:, r : QUADRANTS * ROWS : ROWS, :].rearrange("a q c -> q a c").bitcast(I32))
+
         def load_words(tile, words):
             nc.sync.dma_start(tile[:].bitcast(I32).rearrange("p (a c) -> p a c", a=PASSES), words.bitcast(I32))
 
@@ -115,7 +122,7 @@ def tile_list_photon_triple_coincidence_kernel(
 
         nc.sync.dma_start(offsets[:], offs)
         load_words(w2_raw, w2_words.rearrange("a p c -> p a c"))
-        load_planes_stacked(tab_s, tab_scales)
+        load_planes_apart(tab_s, tab_scales)
         load_table(0)
         load_words(w3_raw, w3_words.rearrange("a p c i -> p a (c i)"))
         load_planes_stacked(w3_s_raw, w3_scales)
@@ -124,7 +131,7 @@ def tile_list_photon_triple_coincidence_kernel(
         load_planes_side_by_side(w2_s_raw, w2_scales)
         deal(w2_w[:].bitcast(U16), w2_raw[:].bitcast(U16), 2)
         nc.vector.tensor_copy(v_s0[:], tab_s[:].indirect(offsets[:]))
-        nc.sync.dma_start(v_s1[0:SHIFTED, :].bitcast(I32), v_s0[ROWS : ROWS + SHIFTED, :].bitcast(I32))
+        nc.sync.dma_start(v_s1[0:SHIFTED, :].bitcast(I32), v_s0[APART:P, :].bitcast(I32))
         load_w1(0, 1)
         w1_pass1 = shared("w1_raw1", "pass1", [P, PACK, H], F32)
         nc.sync.dma_start(w1_pass1[:], w1[K_PASS:K, :].rearrange("(p j) c -> p j c", j=PACK))
@@ -181,7 +188,7 @@ def tile_list_photon_triple_coincidence_kernel(
                 nc.tensor.matmul_mx(
                     out=d3_banks[t, hf][:], lhsT=w3_w[:, dealt_cols(t, a, P)].bitcast(FP8X4),
                     lhsT_scale=w3_s[ROWS * a : P, t * P : (t + 1) * P],
-                    rhs=v_w[a, hf][:].bitcast(FP8X4), rhs_scale=v_s0[ROWS * a : P, hf * HALF : (hf + 1) * HALF],
+                    rhs=v_w[a, hf][:].bitcast(FP8X4), rhs_scale=v_s[a][:, hf * HALF : (hf + 1) * HALF],
                     start=(a == 0), stop=(a == PASSES - 1))
 
         def copy_d3(t, hf):

@@ -235,7 +235,7 @@ def tile_list_photon_triple_coincidence_kernel(
         h_w = [held("h_w%d" % hf, [P, HALF], U32) for hf in range(2)]
         h_s = held("h_s", [P, S], U8)
         gated = [held("gated%d" % hf, [P, NT, HALF], F32) for hf in range(2)]
-        h_b = {}
+        h_b = [held("h_b%d" % hf, [P, HALF * PACK], BF16) for hf in range(2)]
         h = [held("h%d" % hf, [P, PACK, HALF], F32) for hf in range(2)]
         y = [held("y%d" % hf, [P, NT, HALF], F32) for hf in range(2)]
 
@@ -254,12 +254,12 @@ def tile_list_photon_triple_coincidence_kernel(
                     start=(a == 0), stop=(a == PASSES - 1))
             return bank
 
-        def gate_on_gpsimd(hf, i):
+        def gate_on_gpsimd(hf, i, piece=HALF):
             bank = w5_product(hf, i)
             lin = ring.tile([P, HALF], F32, name="lin", bufs=2 * NT)
             nc.scalar.copy(lin[:], bank[:])
-            for lo in range(0, HALF, GATE_PIECE):
-                cols = slice(lo, lo + GATE_PIECE)
+            for lo in range(0, HALF, piece):
+                cols = slice(lo, lo + piece)
                 nc.gpsimd.tensor_tensor(gated[hf][:, i, cols], lin[:, cols], eff_sb[hf][:, i, cols], MULT)
 
         def gate_on_vector(hf, i):
@@ -284,46 +284,29 @@ def tile_list_photon_triple_coincidence_kernel(
 
         def round_h(c):
             hf, in_half = chunk(c)[:2]
-            h_b[c] = held("h_b%d" % c, [P, CHUNK * PACK], BF16)
             nc.scalar.copy(
-                h_b[c][:].rearrange("p (c i t) -> p c t i", i=LINE // 4, t=PACK),
+                h_b[hf][:, PACK * in_half.start : PACK * in_half.stop].rearrange("p (c i t) -> p c t i", i=LINE // 4, t=PACK),
                 h[hf][:, :, in_half].rearrange("p t (c i) -> p c t i", i=LINE // 4))
 
-        def quantize_h(c):
-            hf, in_half, in_list = chunk(c)
-            nc.vector.quantize_mx(out=h_w[hf][:, in_half].bitcast(FP8X4), scales=h_s[:, in_list], in_=h_b[c][:])
-            if in_half.stop == HALF:
-                nc.sync.dma_start(
-                    out_2[0, :, hf * HALF : (hf + 1) * HALF, :].rearrange("p m t -> p (m t)").bitcast(I32),
-                    h_w[hf][:].bitcast(I32))
-            if in_list.stop == S:
+        def quantize_h(hf):
+            cols = slice(hf * HALF, (hf + 1) * HALF)
+            nc.vector.quantize_mx(out=h_w[hf][:].bitcast(FP8X4), scales=h_s[:, cols], in_=h_b[hf][:])
+            nc.sync.dma_start(
+                out_2[0, :, cols, :].rearrange("p m t -> p (m t)").bitcast(I32), h_w[hf][:].bitcast(I32))
+            if cols.stop == S:
                 for q in range(QUADRANTS):
                     nc.scalar.dma_start(
                         out_3[0, ROWS * q : ROWS * (q + 1), :].bitcast(I32),
                         h_s[QUADRANT * q : QUADRANT * q + ROWS, :].bitcast(I32))
 
-        def store_y(c, i0, i1):
-            hf, in_half, in_list = chunk(c)
-            nc.sync.dma_start(
-                out_0[i0 * P : i1 * P, in_list].rearrange("(i p) j -> p i j", p=P), y[hf][:, i0:i1, in_half])
-
-        def make_y(c):
-            hf, in_half, in_list = chunk(c)
-            last = c == CHUNKS - 1
-            for i0 in range(0, NT, 2):
-                i1 = min(i0 + 2, NT)
-                bank = next_bank([P, 2, CHUNK])
-                for i in range(i0, i1):
-                    nc.tensor.matmul_mx(
-                        out=bank[:, i - i0, :], lhsT=w4_w[:, i * P : (i + 1) * P].bitcast(FP8X4),
-                        lhsT_scale=w4_s[:, i * P : (i + 1) * P],
-                        rhs=h_w[hf][:, in_half].bitcast(FP8X4), rhs_scale=h_s[:, in_list], start=True, stop=True)
-                nc.vector.tensor_tensor(
-                    y[hf][:, i0:i1, in_half], bank[:, 0 : i1 - i0, :], gated[hf][:, i0:i1, in_half], ADD)
-                if last:
-                    store_y(c, i0, i1)
-            if not last:
-                store_y(c, 0, NT)
+        def make_y(hf, i):
+            cols = slice(hf * HALF, (hf + 1) * HALF)
+            bank = next_bank([P, HALF])
+            nc.tensor.matmul_mx(
+                out=bank[:], lhsT=w4_w[:, i * P : (i + 1) * P].bitcast(FP8X4), lhsT_scale=w4_s[:, i * P : (i + 1) * P],
+                rhs=h_w[hf][:].bitcast(FP8X4), rhs_scale=h_s[:, cols], start=True, stop=True)
+            nc.vector.tensor_tensor(y[hf][:, i, :], bank[:], gated[hf][:, i, :], ADD)
+            nc.sync.dma_start(out_0[i * P : (i + 1) * P, cols], y[hf][:, i, :])
 
         w3_pass(0, 0)
         w3_pass(1, 0)
@@ -345,21 +328,21 @@ def tile_list_photon_triple_coincidence_kernel(
         gate_on_gpsimd(0, 0)
         make_h(1)
         gate_on_gpsimd(0, 1)
-        gate_on_gpsimd(0, 2)
         round_h(0)
         make_h(2)
+        gate_on_gpsimd(0, 2, GATE_PIECE)
         round_h(1)
-        quantize_h(0)
-        gate_on_gpsimd(1, 0)
-        gate_on_gpsimd(1, 1)
-        make_y(0)
-        quantize_h(1)
         make_h(3)
+        quantize_h(0)
+        gate_on_gpsimd(1, 0, GATE_PIECE)
         round_h(2)
-        make_y(1)
-        round_h(3)
-        quantize_h(2)
         gate_on_vector(1, 2)
-        quantize_h(3)
-        make_y(2)
-        make_y(3)
+        make_y(0, 0)
+        round_h(3)
+        make_y(0, 1)
+        gate_on_gpsimd(1, 1)
+        quantize_h(1)
+        make_y(0, 2)
+        make_y(1, 0)
+        make_y(1, 2)
+        make_y(1, 1)

@@ -24,15 +24,13 @@ QUADRANTS, QUADRANT = 4, 32
 ROWS = 4
 HALF = 512
 CHUNK = 256
-CHUNKS = S // CHUNK
 NT = N // P
 PIECE = H // 2
 LINE = 16
 APART = 16
 SHIFTED = P - APART
-GATE_PIECE = 256
-W4_PARTS = ((0, 256), (256, N))
 BANKS = 8
+WARM_UPS = 2
 ALIGN = 256
 
 
@@ -43,8 +41,7 @@ def tile_list_photon_triple_coincidence_kernel(
     nc = tc.nc
     with ExitStack() as ctx:
         keep = ctx.enter_context(tc.tile_pool(name="keep", bufs=1))
-        ring = ctx.enter_context(tc.tile_pool(name="ring", bufs=3))
-        psum = ctx.enter_context(tc.psum_pool(name="psum", bufs=BANKS))
+        psum = ctx.enter_context(tc.psum_pool(name="psum", bufs=1))
 
         def held(name, shape, dtype):
             return keep.tile(shape, dtype, name=name, align_bytes=ALIGN)
@@ -54,30 +51,28 @@ def tile_list_photon_triple_coincidence_kernel(
 
         banks_used = []
 
-        def next_bank(shape):
-            number = len(banks_used)
-            banks_used.append(number)
-            return psum.tile(shape, F32, name="sum%d" % number, tag="bank")
+        def take_bank(bank, shape):
+            banks_used.append(bank)
+            return psum.tile(shape, F32, name="sum%d" % len(banks_used), tag="bank%d" % bank)
 
         offsets = keep.tile([P, S // 16], U16, name="offsets")
         tab_s = held("tab_s", [P, T], U8)
         tab_w = [held("tab_w%d" % a, [P, T], U32) for a in range(PASSES)]
-        w2_s_raw = held("w2_s_raw", [P, PASSES * H], U8)
         w3_s_raw = shared("w3_s_raw", "picked01", [P, H], U8)
+        w2_s_raw = shared("w2_s_raw", "picked11", [P, PASSES * H], U8)
         w5_s = held("w5_s", [P, PASSES * N], U8)
-        v_s1 = held("v_s1", [P, S], U8)
-        w3_raw = held("w3_raw", [P, PASSES * H], I32)
-        w2_raw = held("w2_raw", [P, PASSES * H * 2], U8)
         v_s0 = held("v_s0", [P, S], U8)
+        v_s1 = held("v_s1", [P, S], U8)
+        w3_raw = [held("w3_raw%d" % a, [P, H], U32) for a in range(PASSES)]
+        w2_raw = held("w2_raw", [P, PASSES * H * 2], U8)
         w5_w = held("w5_w", [P, PASSES * N * 2], U8)
 
         for plane in (tab_s, w3_s_raw, w2_s_raw, v_s1, w5_s):
             nc.vector.memset(plane[:].bitcast(I32), 0)
 
-
-        def load_planes_side_by_side(tile, scales):
-            for q in range(QUADRANTS):
-                nc.sync.dma_start(
+        def load_planes_side_by_side(tile, scales, queue, quadrants=range(QUADRANTS)):
+            for q in quadrants:
+                queue.dma_start(
                     tile[QUADRANT * q : QUADRANT * q + ROWS, :].bitcast(I32).rearrange("r (a c) -> r a c", a=PASSES),
                     scales[:, ROWS * q : ROWS * (q + 1), :].rearrange("a r c -> r a c").bitcast(I32))
 
@@ -93,74 +88,76 @@ def tile_list_photon_triple_coincidence_kernel(
                     tile[r:P:APART, :].bitcast(I32),
                     scales[:, r : QUADRANTS * ROWS : ROWS, :].rearrange("a q c -> q a c").bitcast(I32))
 
-        def load_words(tile, words):
-            nc.sync.dma_start(tile[:].bitcast(I32).rearrange("p (a c) -> p a c", a=PASSES), words.bitcast(I32))
+        def load_words(view, words):
+            nc.sync.dma_start(view.bitcast(I32), words.bitcast(I32))
 
         def load_table(a):
             nc.sync.dma_start(tab_w[a][:].bitcast(I32), tab_words[a].rearrange("p t i -> p (t i)").bitcast(I32))
 
         w1_raw = {}
 
-        def load_w1(a, b):
-            rows = w1[a * K_PASS : (a + 1) * K_PASS, :].rearrange("(p j) c -> p j c", j=PACK)
-            w1_raw[a, b] = shared("w1_raw%d%d" % (a, b), "piece%d%d" % (a, b), [P, PACK, PIECE], F32)
-            nc.sync.dma_start(w1_raw[a, b][:], rows[:, :, b * PIECE : (b + 1) * PIECE])
+        def load_w1_piece(b):
+            rows = w1[0:K_PASS, :].rearrange("(p j) c -> p j c", j=PACK)
+            w1_raw[0, b] = shared("w1_raw0%d" % b, "piece%d" % b, [P, PACK, PIECE], F32)
+            nc.sync.dma_start(w1_raw[0, b][:], rows[:, :, b * PIECE : (b + 1) * PIECE])
 
-        eff_sb = [held("eff%d" % hf, [P, NT, HALF], F32) for hf in range(2)]
+        eff_sb = [held("eff%d" % i, [P, S], F32) for i in range(NT)]
         w4_raw = held("w4_raw", [P, PACK, N], F32)
 
-        def load_eff(hf):
-            nc.sync.dma_start(eff_sb[hf][:], eff[:, hf * HALF : (hf + 1) * HALF].rearrange("(i p) j -> p i j", p=P))
+        nc.sync.dma_start(offsets[:], offs)
+        load_words(w3_raw[0][:], w3_words[0].rearrange("p c i -> p (c i)"))
+        load_planes_apart(tab_s, tab_scales)
+        load_table(0)
+        load_planes_stacked(w3_s_raw, w3_scales)
+        load_planes_side_by_side(w2_s_raw, w2_scales, nc.sync, (0, 1))
+        load_table(1)
+        nc.vector.tensor_copy(v_s0[:], tab_s[:].indirect(offsets[:]))
+        nc.sync.dma_start(v_s1[0:SHIFTED, :].bitcast(I32), v_s0[APART:P, :].bitcast(I32))
+        load_words(w3_raw[1][:], w3_words[1].rearrange("p c i -> p (c i)"))
+        load_words(w2_raw[:].rearrange("p (a c) -> p a c", a=PASSES), w2_words.rearrange("a p c -> p a c"))
+        load_planes_side_by_side(w2_s_raw, w2_scales, nc.sync, (2, 3))
+        load_w1_piece(0)
+        load_w1_piece(1)
+        w1_pass1 = shared("w1_raw1", "pass1", [P, PACK, H], F32)
+        nc.sync.dma_start(w1_pass1[:], w1[K_PASS:K, :].rearrange("(p j) c -> p j c", j=PACK))
+        for b in range(2):
+            w1_raw[1, b] = w1_pass1[:, :, b * PIECE : (b + 1) * PIECE]
+        load_words(w5_w[:].rearrange("p (a c) -> p a c", a=PASSES), w5_words.rearrange("a p c -> p a c"))
+        load_planes_side_by_side(w5_s, w5_scales, nc.gpsimd)
+        nc.sync.dma_start(w4_raw[:], w4.rearrange("(p j) n -> p j n", j=PACK))
+        for i in range(NT):
+            nc.sync.dma_start(eff_sb[i][:], eff[i * P : (i + 1) * P, :])
 
-        def deal(dst, src, size):
+        v_s = [v_s0, v_s1]
+        v_w = {}
+        w3_w = [held("w3_w%d" % a, [P, PACK * P], U32) for a in range(PASSES)]
+        w3_s = held("w3_s", [P, PACK * P], U8)
+        w2_w = held("w2_w", [P, PACK * PASSES * P * 2], U8)
+
+        def deal_lines(dst, src, size):
             run = LINE // size
             nc.vector.tensor_copy(
                 dst.rearrange("p (t g i) -> p g t i", t=PACK, i=run),
                 src.rearrange("p (g i t) -> p g t i", t=PACK, i=run))
 
-        w2_w = held("w2_w", [P, PACK * PASSES * P * 2], U8)
+        def deal_in_order(dst, src):
+            nc.scalar.copy(dst.rearrange("p (t m) -> p m t", t=PACK), src.rearrange("p (m t) -> p m t", t=PACK))
 
-        nc.sync.dma_start(offsets[:], offs)
-        load_words(w2_raw, w2_words.rearrange("a p c -> p a c"))
-        load_planes_apart(tab_s, tab_scales)
-        load_table(0)
-        load_words(w3_raw, w3_words.rearrange("a p c i -> p a (c i)"))
-        load_planes_stacked(w3_s_raw, w3_scales)
-        load_table(1)
-        load_w1(0, 0)
-        load_planes_side_by_side(w2_s_raw, w2_scales)
-        deal(w2_w[:].bitcast(U16), w2_raw[:].bitcast(U16), 2)
-        nc.vector.tensor_copy(v_s0[:], tab_s[:].indirect(offsets[:]))
-        nc.sync.dma_start(v_s1[0:SHIFTED, :].bitcast(I32), v_s0[APART:P, :].bitcast(I32))
-        load_w1(0, 1)
-        w1_pass1 = shared("w1_raw1", "pass1", [P, PACK, H], F32)
-        nc.sync.dma_start(w1_pass1[:], w1[K_PASS:K, :].rearrange("(p j) c -> p j c", j=PACK))
-        for b in range(2):
-            w1_raw[1, b] = w1_pass1[:, :, b * PIECE : (b + 1) * PIECE]
-        load_words(w5_w, w5_words.rearrange("a p c -> p a c"))
-        load_planes_side_by_side(w5_s, w5_scales)
-        nc.sync.dma_start(w4_raw[:], w4.rearrange("(p j) n -> p j n", j=PACK))
-        load_eff(0)
-        load_eff(1)
-
-        v_s = [v_s0, v_s1]
-        v_w = {}
-        w3_w = held("w3_w", [P, PACK * PASSES * P], I32)
-        w3_s = held("w3_s", [P, PACK * P], U8)
-        w2_s = held("w2_s", [P, PACK * PASSES * P], U8)
-
-        def gather_words(a, hf):
-            v_w[a, hf] = shared("v_w%d%d" % (a, hf), "picked%d%d" % (a, hf), [P, HALF], U32)
+        def gather_words(a, hf, tag):
+            v_w[a, hf] = shared("v_w%d%d" % (a, hf), tag, [P, HALF], U32)
             entries = offsets[:, hf * HALF // 16 : (hf + 1) * HALF // 16]
             nc.vector.tensor_copy(v_w[a, hf][:], tab_w[a][:].indirect(entries))
 
-        gather_words(0, 0)
-        deal(w3_w[:], w3_raw[:], 4)
-        deal(w3_s[:], w3_s_raw[:], 1)
-        gather_words(0, 1)
-        gather_words(1, 0)
-        gather_words(1, 1)
-        deal(w2_s[:], w2_s_raw[:], 1)
+        deal_in_order(w3_w[0][:], w3_raw[0][:])
+        deal_in_order(w3_w[1][:], w3_raw[1][:])
+        deal_in_order(w2_w[:].bitcast(U16), w2_raw[:].bitcast(U16))
+        gather_words(0, 0, "picked00")
+        deal_lines(w3_s[:], w3_s_raw[:], 1)
+        gather_words(0, 1, "picked01")
+        gather_words(1, 0, "picked10")
+        w2_s = held("w2_s", [P, PACK * PASSES * P], U8)
+        deal_lines(w2_s[:], w2_s_raw[:], 1)
+        gather_words(1, 1, "picked11")
 
         def dealt_cols(t, a, width):
             return slice((t * PASSES + a) * width, (t * PASSES + a + 1) * width)
@@ -169,37 +166,37 @@ def tile_list_photon_triple_coincidence_kernel(
         w1_w = [held("w1_w%d" % a, [P, H], U32) for a in range(PASSES)]
         w1_s = [held("w1_s%d" % a, [P, H], U8) for a in range(PASSES)]
 
-        def round_w1(a):
-            for b, round_copy in enumerate((nc.scalar.copy, nc.vector.tensor_copy if a else nc.scalar.copy)):
-                places = slice(b * PIECE // PACK, (b + 1) * PIECE // PACK)
-                round_copy(
-                    w1_b[a][:].rearrange("p (t m j) -> p m j t", t=PACK, j=PACK)[:, places],
-                    w1_raw[a, b][:].rearrange("p j (m t) -> p m j t", t=PACK))
+        def round_w1(a, b, round_copy, walk):
+            places = slice(b * PIECE // PACK, (b + 1) * PIECE // PACK)
+            round_copy(
+                w1_b[a][:].rearrange("p (t m j) -> p m " + walk, t=PACK, j=PACK)[:, places],
+                w1_raw[a, b][:].rearrange("p j (m t) -> p m " + walk, t=PACK))
 
         def quantize_w1(a):
             nc.vector.quantize_mx(out=w1_w[a][:].bitcast(FP8X4), scales=w1_s[a][:], in_=w1_b[a][:])
 
         d3_banks, d3, d23 = {}, {}, {}
 
-        def w3_pass(hf, a):
-            for t in range(PACK):
+        def w3_pass(hf, a, slices, first_bank=None):
+            for t in slices:
                 if a == 0:
-                    d3_banks[t, hf] = next_bank([P, HALF])
+                    d3_banks[t, hf] = take_bank(first_bank + t - slices[0], [P, HALF])
                 nc.tensor.matmul_mx(
-                    out=d3_banks[t, hf][:], lhsT=w3_w[:, dealt_cols(t, a, P)].bitcast(FP8X4),
+                    out=d3_banks[t, hf][:], lhsT=w3_w[a][:, t * P : (t + 1) * P].bitcast(FP8X4),
                     lhsT_scale=w3_s[ROWS * a : P, t * P : (t + 1) * P],
                     rhs=v_w[a, hf][:].bitcast(FP8X4), rhs_scale=v_s[a][:, hf * HALF : (hf + 1) * HALF],
                     start=(a == 0), stop=(a == PASSES - 1))
 
+        def hold_d3(name, tag, sums):
+            whole = shared(name, tag, [P, len(sums), HALF], F32)
+            for place, (t, hf) in enumerate(sums):
+                d3[hf, t] = whole[:, place, :]
+
         def copy_d3(t, hf):
-            if t == 0:
-                whole = shared("d3_%d" % hf, "pass1" if hf else "piece01", [P, PACK, HALF], F32)
-                for u in range(PACK):
-                    d3[hf, u] = whole[:, u, :]
             nc.scalar.copy(d3[hf, t], d3_banks[t, hf][:])
 
-        def make_d23(t, hf):
-            bank = next_bank([P, HALF])
+        def make_d23(t, hf, number):
+            bank = take_bank(number, [P, HALF])
             for a in range(PASSES):
                 nc.tensor.matmul_mx(
                     out=bank[:], lhsT=w2_w[:, dealt_cols(t, a, 2 * P)].bitcast(FP4X4),
@@ -208,33 +205,25 @@ def tile_list_photon_triple_coincidence_kernel(
                     start=(a == 0), stop=(a == PASSES - 1))
             if t % 2 == 0:
                 name = "d23_%d%d" % (hf, t // 2)
-                d23[hf, t // 2] = held(name, [P, 2, HALF], F32)
+                d23[hf, t // 2] = shared(name, name if t + hf else "piece0", [P, 2, HALF], F32)
             nc.vector.tensor_tensor(d23[hf, t // 2][:, t % 2, :], bank[:], d3[hf, t], MULT)
 
-        def copy_d3_then_make_d23(slices, hf):
-            for t in slices:
-                copy_d3(t, hf)
-            for t in slices:
-                make_d23(t, hf)
-
         w4_b = held("w4_b", [P, N * PACK], BF16)
-        w4_w = held("w4_w", [P, N], U32)
+        w4_w = {}
         w4_s = held("w4_s", [P, N], U8)
 
         def round_w4():
-            for lo, hi in W4_PARTS:
-                nc.scalar.copy(
-                    w4_b[:, PACK * lo : PACK * hi].rearrange("p (c i j) -> p c j i", i=LINE // 4, j=PACK),
-                    w4_raw[:, :, lo:hi].rearrange("p j (c i) -> p c j i", i=LINE // 4))
+            nc.gpsimd.tensor_copy(
+                w4_b[:].rearrange("p (n j) -> p n j", j=PACK), w4_raw[:].rearrange("p j n -> p n j"))
 
         def quantize_w4():
-            for lo, hi in W4_PARTS:
-                nc.vector.quantize_mx(
-                    out=w4_w[:, lo:hi].bitcast(FP8X4), scales=w4_s[:, lo:hi], in_=w4_b[:, PACK * lo : PACK * hi])
+            w4_w[0] = shared("w4_w", "pass1", [P, N], U32)
+            nc.vector.quantize_mx(out=w4_w[0][:].bitcast(FP8X4), scales=w4_s[:], in_=w4_b[:])
 
-        h_w = [held("h_w%d" % hf, [P, HALF], U32) for hf in range(2)]
+        h_w = {}
         h_s = held("h_s", [P, S], U8)
-        gated = [held("gated%d" % hf, [P, NT, HALF], F32) for hf in range(2)]
+        lin = [held("lin%d" % hf, [P, NT, HALF], F32) for hf in range(2)]
+        gated = {}
         h_b = [held("h_b%d" % hf, [P, HALF * PACK], BF16) for hf in range(2)]
         h = [held("h%d" % hf, [P, PACK, HALF], F32) for hf in range(2)]
         y = [held("y%d" % hf, [P, NT, HALF], F32) for hf in range(2)]
@@ -243,8 +232,8 @@ def tile_list_photon_triple_coincidence_kernel(
             hf, lo = divmod(c * CHUNK, HALF)
             return hf, slice(lo, lo + CHUNK), slice(c * CHUNK, (c + 1) * CHUNK)
 
-        def w5_product(hf, i):
-            bank = next_bank([P, HALF])
+        def gate(hf, i, number):
+            bank = take_bank(number, [P, HALF])
             for a in range(PASSES):
                 first = a * N + i * P
                 nc.tensor.matmul_mx(
@@ -252,35 +241,30 @@ def tile_list_photon_triple_coincidence_kernel(
                     lhsT_scale=w5_s[:, first : first + P],
                     rhs=v_w[a, hf][:].bitcast(FP8X4), rhs_scale=v_s[a][:, hf * HALF : (hf + 1) * HALF],
                     start=(a == 0), stop=(a == PASSES - 1))
-            return bank
+            nc.scalar.copy(lin[hf][:, i, :], bank[:])
+            gated[hf, i] = shared("gated%d%d" % (hf, i), "gated%d%d" % (hf, i), [P, HALF], F32)
+            nc.gpsimd.tensor_tensor(
+                gated[hf, i][:], lin[hf][:, i, :], eff_sb[i][:, hf * HALF : (hf + 1) * HALF], MULT)
 
-        def gate_on_gpsimd(hf, i, piece=HALF):
-            bank = w5_product(hf, i)
-            lin = ring.tile([P, HALF], F32, name="lin", bufs=2 * NT)
-            nc.scalar.copy(lin[:], bank[:])
-            for lo in range(0, HALF, piece):
-                cols = slice(lo, lo + piece)
-                nc.gpsimd.tensor_tensor(gated[hf][:, i, cols], lin[:, cols], eff_sb[hf][:, i, cols], MULT)
-
-        def gate_on_vector(hf, i):
-            bank = w5_product(hf, i)
-            nc.vector.tensor_tensor(gated[hf][:, i, :], bank[:], eff_sb[hf][:, i, :], MULT)
-
-        def make_h(c):
+        def make_h_pair(c, pair, number):
             hf, in_half, in_list = chunk(c)
+            bank = take_bank(number, [P, 2, CHUNK])
+            for e in range(2):
+                t = 2 * pair + e
+                for a in range(PASSES):
+                    nc.tensor.matmul_mx(
+                        out=bank[:, e, :], lhsT=w1_w[a][:, t * P : (t + 1) * P].bitcast(FP8X4),
+                        lhsT_scale=w1_s[a][:, t * P : (t + 1) * P],
+                        rhs=v_w[a, hf][:, in_half].bitcast(FP8X4), rhs_scale=v_s[a][:, in_list],
+                        start=(a == 0), stop=(a == PASSES - 1))
+            nc.vector.tensor_tensor(
+                h[hf][:, 2 * pair : 2 * pair + 2, in_half], bank[:], d23[hf, pair][:, :, in_half], MULT)
+            if pair == 1:
+                nc.sync.dma_start(out_1[:, in_list].rearrange("(p t) j -> p t j", t=PACK), h[hf][:, :, in_half])
+
+        def make_h(c, numbers):
             for pair in range(PACK // 2):
-                bank = next_bank([P, 2, CHUNK])
-                for e in range(2):
-                    t = 2 * pair + e
-                    for a in range(PASSES):
-                        nc.tensor.matmul_mx(
-                            out=bank[:, e, :], lhsT=w1_w[a][:, t * P : (t + 1) * P].bitcast(FP8X4),
-                            lhsT_scale=w1_s[a][:, t * P : (t + 1) * P],
-                            rhs=v_w[a, hf][:, in_half].bitcast(FP8X4), rhs_scale=v_s[a][:, in_list],
-                            start=(a == 0), stop=(a == PASSES - 1))
-                nc.vector.tensor_tensor(
-                    h[hf][:, 2 * pair : 2 * pair + 2, in_half], bank[:], d23[hf, pair][:, :, in_half], MULT)
-            nc.sync.dma_start(out_1[:, in_list].rearrange("(p t) j -> p t j", t=PACK), h[hf][:, :, in_half])
+                make_h_pair(c, pair, numbers[pair])
 
         def round_h(c):
             hf, in_half = chunk(c)[:2]
@@ -290,6 +274,7 @@ def tile_list_photon_triple_coincidence_kernel(
 
         def quantize_h(hf):
             cols = slice(hf * HALF, (hf + 1) * HALF)
+            h_w[hf] = shared("h_w%d" % hf, "gated01" if hf else "h_w0", [P, HALF], U32)
             nc.vector.quantize_mx(out=h_w[hf][:].bitcast(FP8X4), scales=h_s[:, cols], in_=h_b[hf][:])
             nc.sync.dma_start(
                 out_2[0, :, cols, :].rearrange("p m t -> p (m t)").bitcast(I32), h_w[hf][:].bitcast(I32))
@@ -299,50 +284,67 @@ def tile_list_photon_triple_coincidence_kernel(
                         out_3[0, ROWS * q : ROWS * (q + 1), :].bitcast(I32),
                         h_s[QUADRANT * q : QUADRANT * q + ROWS, :].bitcast(I32))
 
-        def make_y(hf, i):
+        def make_y(hf, i, number):
             cols = slice(hf * HALF, (hf + 1) * HALF)
-            bank = next_bank([P, HALF])
+            bank = take_bank(number, [P, HALF])
             nc.tensor.matmul_mx(
-                out=bank[:], lhsT=w4_w[:, i * P : (i + 1) * P].bitcast(FP8X4), lhsT_scale=w4_s[:, i * P : (i + 1) * P],
+                out=bank[:], lhsT=w4_w[0][:, i * P : (i + 1) * P].bitcast(FP8X4), lhsT_scale=w4_s[:, i * P : (i + 1) * P],
                 rhs=h_w[hf][:].bitcast(FP8X4), rhs_scale=h_s[:, cols], start=True, stop=True)
-            nc.vector.tensor_tensor(y[hf][:, i, :], bank[:], gated[hf][:, i, :], ADD)
+            nc.vector.tensor_tensor(y[hf][:, i, :], bank[:], gated[hf, i][:], ADD)
             nc.sync.dma_start(out_0[i * P : (i + 1) * P, cols], y[hf][:, i, :])
 
-        w3_pass(0, 0)
-        w3_pass(1, 0)
-        w3_pass(0, 1)
-        round_w1(0)
-        quantize_w1(0)
-        copy_d3_then_make_d23((0, 1), 0)
-        w3_pass(1, 1)
-        for t in (2, 3):
+        warm = take_bank(BANKS - 1, [P, HALF])
+        for unused in range(WARM_UPS):
+            nc.tensor.matmul_mx(
+                out=warm[:], lhsT=w3_raw[0][:, 0:P].bitcast(FP8X4), lhsT_scale=w3_s_raw[:, 0:P],
+                rhs=w3_raw[0][:].bitcast(FP8X4), rhs_scale=w3_s_raw[:], start=True, stop=True)
+        w3_pass(0, 0, (0, 1, 2, 3), 0)
+        w3_pass(1, 0, (0, 1, 2), 4)
+        w3_pass(0, 1, (0, 1, 2, 3))
+        round_w1(0, 0, nc.vector.tensor_copy, "j t")
+        hold_d3("d3_a", "d3_a", ((0, 0), (1, 0)))
+        for t, number in ((0, 7), (1, 0)):
             copy_d3(t, 0)
-        round_w1(1)
-        for t in (2, 3):
-            make_d23(t, 0)
+            make_d23(t, 0, number)
+        w3_pass(1, 1, (0, 1, 2))
+        round_w1(0, 1, nc.scalar.copy, "j t")
+        quantize_w1(0)
+        hold_d3("d3_b", "piece1", ((2, 0), (3, 0), (0, 1)))
+        for t, number in ((2, 1), (3, 7)):
+            copy_d3(t, 0)
+            make_d23(t, 0, number)
+        copy_d3(0, 1)
+        make_d23(0, 1, 2)
+        w3_pass(1, 0, (3,), 3)
+        w3_pass(1, 1, (3,))
+        round_w1(1, 0, nc.scalar.copy, "j t")
+        round_w1(1, 1, nc.vector.tensor_copy, "j t")
         quantize_w1(1)
-        copy_d3_then_make_d23(range(PACK), 1)
+        hold_d3("d3_c", "pass1", ((1, 1), (2, 1), (3, 1)))
+        for t, number in ((1, 0), (2, 1), (3, 7)):
+            copy_d3(t, 1)
+            make_d23(t, 1, number)
         round_w4()
+        gate(0, 0, 4)
+        gate(0, 1, 2)
+        make_h(0, (5, 6))
         quantize_w4()
-        make_h(0)
-        gate_on_gpsimd(0, 0)
-        make_h(1)
-        gate_on_gpsimd(0, 1)
+        gate(0, 2, 0)
+        make_h(1, (3, 1))
         round_h(0)
-        make_h(2)
-        gate_on_gpsimd(0, 2, GATE_PIECE)
+        make_h(2, (7, 4))
         round_h(1)
-        make_h(3)
+        gate(1, 0, 5)
         quantize_h(0)
-        gate_on_gpsimd(1, 0, GATE_PIECE)
+        make_h(3, (2, 6))
         round_h(2)
-        gate_on_vector(1, 2)
-        make_y(0, 0)
+        gate(1, 1, 7)
         round_h(3)
-        make_y(0, 1)
-        gate_on_gpsimd(1, 1)
+        gate(1, 2, 2)
+        make_y(0, 0, 0)
+        make_y(0, 1, 3)
         quantize_h(1)
-        make_y(0, 2)
-        make_y(1, 0)
-        make_y(1, 2)
-        make_y(1, 1)
+        make_y(0, 2, 1)
+        make_y(1, 0, 4)
+        make_y(1, 1, 5)
+        make_y(1, 2, 6)

@@ -29,6 +29,8 @@ PIECE = H // 2
 LINE = 16
 APART = 16
 SHIFTED = P - APART
+GATE_PIECE = 256
+W4_PIECE = 96
 BANKS = 8
 WARM_UPS = 2
 ALIGN = 256
@@ -41,6 +43,7 @@ def tile_list_photon_triple_coincidence_kernel(
     nc = tc.nc
     with ExitStack() as ctx:
         keep = ctx.enter_context(tc.tile_pool(name="keep", bufs=1))
+        placed = ctx.enter_context(tc.tile_pool(name="placed", bufs=1))
         psum = ctx.enter_context(tc.psum_pool(name="psum", bufs=1))
 
         def held(name, shape, dtype):
@@ -59,19 +62,19 @@ def tile_list_photon_triple_coincidence_kernel(
         tab_s = held("tab_s", [P, T], U8)
         tab_w = [held("tab_w%d" % a, [P, T], U32) for a in range(PASSES)]
         w3_s_raw = shared("w3_s_raw", "picked01", [P, H], U8)
-        w2_s_raw = shared("w2_s_raw", "picked11", [P, PASSES * H], U8)
+        w2_s_raw = placed.tile([P, PASSES * H], U8, name="w2_s_raw", offset=0, align_bytes=ALIGN)
         w5_s = held("w5_s", [P, PASSES * N], U8)
         v_s0 = held("v_s0", [P, S], U8)
         v_s1 = held("v_s1", [P, S], U8)
         w3_raw = [held("w3_raw%d" % a, [P, H], U32) for a in range(PASSES)]
-        w2_raw = held("w2_raw", [P, PASSES * H * 2], U8)
+        w2_raw = placed.tile([P, PASSES * H * 2], U8, name="w2_raw", offset=PASSES * H, align_bytes=ALIGN)
         w5_w = held("w5_w", [P, PASSES * N * 2], U8)
 
         for plane in (tab_s, w3_s_raw, w2_s_raw, v_s1, w5_s):
             nc.vector.memset(plane[:].bitcast(I32), 0)
 
-        def load_planes_side_by_side(tile, scales, queue, quadrants=range(QUADRANTS)):
-            for q in quadrants:
+        def load_planes_side_by_side(tile, scales, queue):
+            for q in range(QUADRANTS):
                 queue.dma_start(
                     tile[QUADRANT * q : QUADRANT * q + ROWS, :].bitcast(I32).rearrange("r (a c) -> r a c", a=PASSES),
                     scales[:, ROWS * q : ROWS * (q + 1), :].rearrange("a r c -> r a c").bitcast(I32))
@@ -109,13 +112,12 @@ def tile_list_photon_triple_coincidence_kernel(
         load_planes_apart(tab_s, tab_scales)
         load_table(0)
         load_planes_stacked(w3_s_raw, w3_scales)
-        load_planes_side_by_side(w2_s_raw, w2_scales, nc.sync, (0, 1))
+        load_words(w3_raw[1][:], w3_words[1].rearrange("p c i -> p (c i)"))
         load_table(1)
+        load_words(w2_raw[:].rearrange("p (a c) -> p a c", a=PASSES), w2_words.rearrange("a p c -> p a c"))
+        load_planes_side_by_side(w2_s_raw, w2_scales, nc.sync)
         nc.vector.tensor_copy(v_s0[:], tab_s[:].indirect(offsets[:]))
         nc.sync.dma_start(v_s1[0:SHIFTED, :].bitcast(I32), v_s0[APART:P, :].bitcast(I32))
-        load_words(w3_raw[1][:], w3_words[1].rearrange("p c i -> p (c i)"))
-        load_words(w2_raw[:].rearrange("p (a c) -> p a c", a=PASSES), w2_words.rearrange("a p c -> p a c"))
-        load_planes_side_by_side(w2_s_raw, w2_scales, nc.sync, (2, 3))
         load_w1_piece(0)
         load_w1_piece(1)
         w1_pass1 = shared("w1_raw1", "pass1", [P, PACK, H], F32)
@@ -144,7 +146,10 @@ def tile_list_photon_triple_coincidence_kernel(
             nc.scalar.copy(dst.rearrange("p (t m) -> p m t", t=PACK), src.rearrange("p (m t) -> p m t", t=PACK))
 
         def gather_words(a, hf, tag):
-            v_w[a, hf] = shared("v_w%d%d" % (a, hf), tag, [P, HALF], U32)
+            if tag:
+                v_w[a, hf] = shared("v_w%d%d" % (a, hf), tag, [P, HALF], U32)
+            else:
+                v_w[a, hf] = placed.tile([P, HALF], U32, name="v_w11", offset=0, align_bytes=ALIGN)
             entries = offsets[:, hf * HALF // 16 : (hf + 1) * HALF // 16]
             nc.vector.tensor_copy(v_w[a, hf][:], tab_w[a][:].indirect(entries))
 
@@ -157,7 +162,7 @@ def tile_list_photon_triple_coincidence_kernel(
         gather_words(1, 0, "picked10")
         w2_s = held("w2_s", [P, PACK * PASSES * P], U8)
         deal_lines(w2_s[:], w2_s_raw[:], 1)
-        gather_words(1, 1, "picked11")
+        gather_words(1, 1, None)
 
         def dealt_cols(t, a, width):
             return slice((t * PASSES + a) * width, (t * PASSES + a + 1) * width)
@@ -208,13 +213,15 @@ def tile_list_photon_triple_coincidence_kernel(
                 d23[hf, t // 2] = shared(name, name if t + hf else "piece0", [P, 2, HALF], F32)
             nc.vector.tensor_tensor(d23[hf, t // 2][:, t % 2, :], bank[:], d3[hf, t], MULT)
 
-        w4_b = held("w4_b", [P, N * PACK], BF16)
+        w4_b = shared("w4_b", "w4_b", [P, N * PACK], BF16)
         w4_w = {}
         w4_s = held("w4_s", [P, N], U8)
 
         def round_w4():
-            nc.gpsimd.tensor_copy(
-                w4_b[:].rearrange("p (n j) -> p n j", j=PACK), w4_raw[:].rearrange("p j n -> p n j"))
+            for lo in range(0, N, W4_PIECE):
+                nc.gpsimd.tensor_copy(
+                    w4_b[:, PACK * lo : PACK * (lo + W4_PIECE)].rearrange("p (n j) -> p n j", j=PACK),
+                    w4_raw[:, :, lo : lo + W4_PIECE].rearrange("p j n -> p n j"))
 
         def quantize_w4():
             w4_w[0] = shared("w4_w", "pass1", [P, N], U32)
@@ -224,7 +231,7 @@ def tile_list_photon_triple_coincidence_kernel(
         h_s = held("h_s", [P, S], U8)
         lin = [held("lin%d" % hf, [P, NT, HALF], F32) for hf in range(2)]
         gated = {}
-        h_b = [held("h_b%d" % hf, [P, HALF * PACK], BF16) for hf in range(2)]
+        h_b = [shared("h_b%d" % hf, "h_b%d" % hf, [P, HALF * PACK], BF16) for hf in range(2)]
         h = [held("h%d" % hf, [P, PACK, HALF], F32) for hf in range(2)]
         y = [held("y%d" % hf, [P, NT, HALF], F32) for hf in range(2)]
 
@@ -232,7 +239,7 @@ def tile_list_photon_triple_coincidence_kernel(
             hf, lo = divmod(c * CHUNK, HALF)
             return hf, slice(lo, lo + CHUNK), slice(c * CHUNK, (c + 1) * CHUNK)
 
-        def gate(hf, i, number):
+        def w5_sum(hf, i, number):
             bank = take_bank(number, [P, HALF])
             for a in range(PASSES):
                 first = a * N + i * P
@@ -242,9 +249,17 @@ def tile_list_photon_triple_coincidence_kernel(
                     rhs=v_w[a, hf][:].bitcast(FP8X4), rhs_scale=v_s[a][:, hf * HALF : (hf + 1) * HALF],
                     start=(a == 0), stop=(a == PASSES - 1))
             nc.scalar.copy(lin[hf][:, i, :], bank[:])
-            gated[hf, i] = shared("gated%d%d" % (hf, i), "gated%d%d" % (hf, i), [P, HALF], F32)
-            nc.gpsimd.tensor_tensor(
-                gated[hf, i][:], lin[hf][:, i, :], eff_sb[i][:, hf * HALF : (hf + 1) * HALF], MULT)
+
+        def hold_gated(name, tag, sums):
+            whole = shared(name, tag, [P, len(sums), HALF], F32)
+            for place, key in enumerate(sums):
+                gated[key] = whole[:, place, :]
+
+        def gate(hf, i, piece=HALF):
+            for lo in range(0, HALF, piece):
+                nc.gpsimd.tensor_tensor(
+                    gated[hf, i][:, lo : lo + piece], lin[hf][:, i, lo : lo + piece],
+                    eff_sb[i][:, hf * HALF + lo : hf * HALF + lo + piece], MULT)
 
         def make_h_pair(c, pair, number):
             hf, in_half, in_list = chunk(c)
@@ -274,7 +289,7 @@ def tile_list_photon_triple_coincidence_kernel(
 
         def quantize_h(hf):
             cols = slice(hf * HALF, (hf + 1) * HALF)
-            h_w[hf] = shared("h_w%d" % hf, "gated01" if hf else "h_w0", [P, HALF], U32)
+            h_w[hf] = shared("h_w%d" % hf, "w4_b" if hf else "h_w0", [P, HALF], U32)
             nc.vector.quantize_mx(out=h_w[hf][:].bitcast(FP8X4), scales=h_s[:, cols], in_=h_b[hf][:])
             nc.sync.dma_start(
                 out_2[0, :, cols, :].rearrange("p m t -> p (m t)").bitcast(I32), h_w[hf][:].bitcast(I32))
@@ -290,7 +305,7 @@ def tile_list_photon_triple_coincidence_kernel(
             nc.tensor.matmul_mx(
                 out=bank[:], lhsT=w4_w[0][:, i * P : (i + 1) * P].bitcast(FP8X4), lhsT_scale=w4_s[:, i * P : (i + 1) * P],
                 rhs=h_w[hf][:].bitcast(FP8X4), rhs_scale=h_s[:, cols], start=True, stop=True)
-            nc.vector.tensor_tensor(y[hf][:, i, :], bank[:], gated[hf, i][:], ADD)
+            nc.vector.tensor_tensor(y[hf][:, i, :], bank[:], gated[hf, i], ADD)
             nc.sync.dma_start(out_0[i * P : (i + 1) * P, cols], y[hf][:, i, :])
 
         warm = take_bank(BANKS - 1, [P, HALF])
@@ -325,25 +340,35 @@ def tile_list_photon_triple_coincidence_kernel(
             copy_d3(t, 1)
             make_d23(t, 1, number)
         round_w4()
-        gate(0, 0, 4)
-        gate(0, 1, 2)
-        make_h(0, (5, 6))
+        w5_sum(0, 0, 4)
+        w5_sum(0, 1, 2)
         quantize_w4()
-        gate(0, 2, 0)
+        make_h(0, (5, 6))
+        hold_gated("gated_a", "w4_b", ((0, 0), (0, 1)))
+        gate(0, 0)
+        gate(0, 1)
+        w5_sum(0, 2, 0)
+        hold_gated("gated_b", "gated_b", ((0, 2), (1, 1)))
+        gate(0, 2, GATE_PIECE)
         make_h(1, (3, 1))
         round_h(0)
         make_h(2, (7, 4))
         round_h(1)
-        gate(1, 0, 5)
+        w5_sum(1, 0, 5)
         quantize_h(0)
+        hold_gated("gated_c", "h_b0", ((1, 0),))
+        gate(1, 0)
         make_h(3, (2, 6))
         round_h(2)
-        gate(1, 1, 7)
+        w5_sum(1, 1, 7)
+        gate(1, 1, GATE_PIECE)
         round_h(3)
-        gate(1, 2, 2)
+        w5_sum(1, 2, 2)
         make_y(0, 0, 0)
         make_y(0, 1, 3)
         quantize_h(1)
+        hold_gated("gated_d", "h_b1", ((1, 2),))
+        gate(1, 2)
         make_y(0, 2, 1)
         make_y(1, 0, 4)
         make_y(1, 1, 5)

@@ -30,7 +30,6 @@ LINE = 16
 APART = 16
 SHIFTED = P - APART
 GATE_PIECE = 256
-W4_PIECE = 96
 BANKS = 8
 WARM_UPS = 2
 ALIGN = 256
@@ -105,7 +104,7 @@ def tile_list_photon_triple_coincidence_kernel(
             nc.sync.dma_start(w1_raw[0, b][:], rows[:, :, b * PIECE : (b + 1) * PIECE])
 
         eff_sb = [held("eff%d" % i, [P, S], F32) for i in range(NT)]
-        w4_raw = held("w4_raw", [P, PACK, N], F32)
+        w4_raw = shared("w4_raw", "w4_raw", [P, PACK, N], F32)
 
         nc.sync.dma_start(offsets[:], offs)
         load_words(w3_raw[0][:], w3_words[0].rearrange("p c i -> p (c i)"))
@@ -218,10 +217,9 @@ def tile_list_photon_triple_coincidence_kernel(
         w4_s = held("w4_s", [P, N], U8)
 
         def round_w4():
-            for lo in range(0, N, W4_PIECE):
-                nc.gpsimd.tensor_copy(
-                    w4_b[:, PACK * lo : PACK * (lo + W4_PIECE)].rearrange("p (n j) -> p n j", j=PACK),
-                    w4_raw[:, :, lo : lo + W4_PIECE].rearrange("p j n -> p n j"))
+            nc.scalar.copy(
+                w4_b[:].rearrange("p (c i j) -> p c j i", i=LINE // 4, j=PACK),
+                w4_raw[:].rearrange("p j (c i) -> p c j i", i=LINE // 4))
 
         def quantize_w4():
             w4_w[0] = shared("w4_w", "pass1", [P, N], U32)
@@ -229,7 +227,7 @@ def tile_list_photon_triple_coincidence_kernel(
 
         h_w = {}
         h_s = held("h_s", [P, S], U8)
-        lin = [held("lin%d" % hf, [P, NT, HALF], F32) for hf in range(2)]
+        lin = {}
         gated = {}
         h_b = [shared("h_b%d" % hf, "h_b%d" % hf, [P, HALF * PACK], BF16) for hf in range(2)]
         h = [held("h%d" % hf, [P, PACK, HALF], F32) for hf in range(2)]
@@ -239,7 +237,7 @@ def tile_list_photon_triple_coincidence_kernel(
             hf, lo = divmod(c * CHUNK, HALF)
             return hf, slice(lo, lo + CHUNK), slice(c * CHUNK, (c + 1) * CHUNK)
 
-        def w5_sum(hf, i, number):
+        def w5_product(hf, i, number):
             bank = take_bank(number, [P, HALF])
             for a in range(PASSES):
                 first = a * N + i * P
@@ -248,7 +246,17 @@ def tile_list_photon_triple_coincidence_kernel(
                     lhsT_scale=w5_s[:, first : first + P],
                     rhs=v_w[a, hf][:].bitcast(FP8X4), rhs_scale=v_s[a][:, hf * HALF : (hf + 1) * HALF],
                     start=(a == 0), stop=(a == PASSES - 1))
+            return bank
+
+        def w5_sum(hf, i, number):
+            bank = w5_product(hf, i, number)
+            if i == 0:
+                lin[hf] = shared("lin%d" % hf, "lin1" if hf else "w4_raw", [P, NT, HALF], F32)
             nc.scalar.copy(lin[hf][:, i, :], bank[:])
+
+        def gate_on_vector(hf, i, number):
+            bank = w5_product(hf, i, number)
+            nc.vector.tensor_tensor(gated[hf, i], bank[:], eff_sb[i][:, hf * HALF : (hf + 1) * HALF], MULT)
 
         def hold_gated(name, tag, sums):
             whole = shared(name, tag, [P, len(sums), HALF], F32)
@@ -317,59 +325,60 @@ def tile_list_photon_triple_coincidence_kernel(
         w3_pass(1, 0, (0, 1, 2), 4)
         w3_pass(0, 1, (0, 1, 2, 3))
         round_w1(0, 0, nc.vector.tensor_copy, "j t")
-        hold_d3("d3_a", "d3_a", ((0, 0), (1, 0)))
+        hold_d3("d3_a", "d3_a", ((0, 0), (1, 0), (2, 0), (3, 0)))
         for t, number in ((0, 7), (1, 0)):
             copy_d3(t, 0)
             make_d23(t, 0, number)
         w3_pass(1, 1, (0, 1, 2))
+        for t in (2, 3):
+            copy_d3(t, 0)
+            make_d23(t, 0, t - 1)
         round_w1(0, 1, nc.scalar.copy, "j t")
         quantize_w1(0)
-        hold_d3("d3_b", "piece1", ((2, 0), (3, 0), (0, 1)))
-        for t, number in ((2, 1), (3, 7)):
-            copy_d3(t, 0)
-            make_d23(t, 0, number)
+        hold_d3("d3_b", "piece1", ((0, 1), (1, 1)))
         copy_d3(0, 1)
-        make_d23(0, 1, 2)
+        make_d23(0, 1, 7)
         w3_pass(1, 0, (3,), 3)
         w3_pass(1, 1, (3,))
-        round_w1(1, 0, nc.scalar.copy, "j t")
         round_w1(1, 1, nc.vector.tensor_copy, "j t")
+        copy_d3(1, 1)
+        make_d23(1, 1, 0)
+        round_w1(1, 0, nc.scalar.copy, "j t")
         quantize_w1(1)
-        hold_d3("d3_c", "pass1", ((1, 1), (2, 1), (3, 1)))
-        for t, number in ((1, 0), (2, 1), (3, 7)):
+        hold_d3("d3_c", "pass1", ((2, 1), (3, 1)))
+        for t in (2, 3):
             copy_d3(t, 1)
-            make_d23(t, 1, number)
+            make_d23(t, 1, t - 1)
         round_w4()
-        w5_sum(0, 0, 4)
-        w5_sum(0, 1, 2)
+        w5_sum(0, 0, 7)
+        w5_sum(0, 1, 4)
+        make_h(0, (5, 0))
+        make_h_pair(1, 0, 6)
         quantize_w4()
-        make_h(0, (5, 6))
         hold_gated("gated_a", "w4_b", ((0, 0), (0, 1)))
         gate(0, 0)
         gate(0, 1)
-        w5_sum(0, 2, 0)
-        hold_gated("gated_b", "gated_b", ((0, 2), (1, 1)))
-        gate(0, 2, GATE_PIECE)
-        make_h(1, (3, 1))
+        make_h_pair(1, 1, 3)
         round_h(0)
-        make_h(2, (7, 4))
+        hold_gated("gated_b", "gated_b", ((0, 2), (1, 0), (1, 1)))
+        make_h(2, (2, 5))
+        w5_sum(0, 2, 6)
+        gate(0, 2, GATE_PIECE)
         round_h(1)
-        w5_sum(1, 0, 5)
+        make_h(3, (1, 0))
+        w5_sum(1, 0, 2)
+        gate(1, 0, GATE_PIECE)
         quantize_h(0)
-        hold_gated("gated_c", "h_b0", ((1, 0),))
-        gate(1, 0)
-        make_h(3, (2, 6))
         round_h(2)
-        w5_sum(1, 1, 7)
-        gate(1, 1, GATE_PIECE)
+        hold_gated("gated_c", "h_b0", ((1, 2),))
+        gate_on_vector(1, 2, 5)
+        make_y(0, 0, 4)
         round_h(3)
-        w5_sum(1, 2, 2)
-        make_y(0, 0, 0)
-        make_y(0, 1, 3)
+        w5_sum(1, 1, 0)
+        gate(1, 1)
+        make_y(0, 1, 7)
         quantize_h(1)
-        hold_gated("gated_d", "h_b1", ((1, 2),))
-        gate(1, 2)
-        make_y(0, 2, 1)
-        make_y(1, 0, 4)
-        make_y(1, 1, 5)
-        make_y(1, 2, 6)
+        make_y(0, 2, 3)
+        make_y(1, 0, 6)
+        make_y(1, 2, 1)
+        make_y(1, 1, 2)

@@ -65,11 +65,11 @@ def tile_list_photon_triple_coincidence_kernel(
         w5_s = held("w5_s", [P, PASSES * N], U8)
         v_s0 = held("v_s0", [P, S], U8)
         v_s1 = held("v_s1", [P, S], U8)
-        w3_raw = [held("w3_raw%d" % a, [P, H], U32) for a in range(PASSES)]
+        w3_raw = [shared("w3_raw%d" % a, "w3_raw%d" % a, [P, H], U32) for a in range(PASSES)]
         w2_raw = placed.tile([P, PASSES * H * 2], U8, name="w2_raw", offset=PASSES * H, align_bytes=ALIGN)
         w5_w = held("w5_w", [P, PASSES * N * 2], U8)
 
-        for plane in (tab_s, w3_s_raw, w2_s_raw, v_s1, w5_s):
+        for plane in (tab_s, w2_s_raw, w3_s_raw, v_s1, w5_s):
             nc.vector.memset(plane[:].bitcast(I32), 0)
 
         def load_planes_side_by_side(tile, scales, queue):
@@ -111,10 +111,10 @@ def tile_list_photon_triple_coincidence_kernel(
         load_planes_apart(tab_s, tab_scales)
         load_table(0)
         load_planes_stacked(w3_s_raw, w3_scales)
-        load_words(w3_raw[1][:], w3_words[1].rearrange("p c i -> p (c i)"))
         load_table(1)
+        load_words(w3_raw[1][:], w3_words[1].rearrange("p c i -> p (c i)"))
         load_words(w2_raw[:].rearrange("p (a c) -> p a c", a=PASSES), w2_words.rearrange("a p c -> p a c"))
-        load_planes_side_by_side(w2_s_raw, w2_scales, nc.sync)
+        load_planes_side_by_side(w2_s_raw, w2_scales, nc.gpsimd)
         nc.vector.tensor_copy(v_s0[:], tab_s[:].indirect(offsets[:]))
         nc.sync.dma_start(v_s1[0:SHIFTED, :].bitcast(I32), v_s0[APART:P, :].bitcast(I32))
         load_w1_piece(0)
@@ -159,7 +159,7 @@ def tile_list_photon_triple_coincidence_kernel(
         deal_lines(w3_s[:], w3_s_raw[:], 1)
         gather_words(0, 1, "picked01")
         gather_words(1, 0, "picked10")
-        w2_s = held("w2_s", [P, PACK * PASSES * P], U8)
+        w2_s = shared("w2_s", "w3_raw1", [P, PACK * PASSES * P], U8)
         deal_lines(w2_s[:], w2_s_raw[:], 1)
         gather_words(1, 1, None)
 
@@ -360,24 +360,25 @@ def tile_list_photon_triple_coincidence_kernel(
         gate(0, 1)
         make_h_pair(1, 1, 3)
         round_h(0)
-        hold_gated("gated_b", "gated_b", ((0, 2), (1, 0), (1, 1)))
+        hold_gated("gated_b", "gated_b", ((0, 2),))
         make_h(2, (2, 5))
         w5_sum(0, 2, 6)
         gate(0, 2, GATE_PIECE)
         round_h(1)
         make_h(3, (1, 0))
         w5_sum(1, 0, 2)
-        gate(1, 0, GATE_PIECE)
         quantize_h(0)
         round_h(2)
-        hold_gated("gated_c", "h_b0", ((1, 2),))
+        hold_gated("gated_c", "h_b0", ((1, 0), (1, 2)))
+        gate(1, 0)
         gate_on_vector(1, 2, 5)
         make_y(0, 0, 4)
         round_h(3)
         w5_sum(1, 1, 0)
-        gate(1, 1)
         make_y(0, 1, 7)
         quantize_h(1)
+        hold_gated("gated_d", "h_b1", ((1, 1),))
+        gate(1, 1)
         make_y(0, 2, 3)
         make_y(1, 0, 6)
         make_y(1, 2, 1)

@@ -69,18 +69,18 @@ def tile_list_photon_triple_coincidence_kernel(
         w2_raw = placed.tile([P, PASSES * H * 2], U8, name="w2_raw", offset=PASSES * H, align_bytes=ALIGN)
         w5_w = held("w5_w", [P, PASSES * N * 2], U8)
 
-        for plane in (tab_s, w2_s_raw, w3_s_raw, v_s1, w5_s):
+        for plane in (tab_s, w3_s_raw, w2_s_raw, v_s1, w5_s):
             nc.vector.memset(plane[:].bitcast(I32), 0)
 
-        def load_planes_side_by_side(tile, scales, queue):
-            for q in range(QUADRANTS):
+        def load_planes_side_by_side(tile, scales, queue, quadrants=range(QUADRANTS)):
+            for q in quadrants:
                 queue.dma_start(
                     tile[QUADRANT * q : QUADRANT * q + ROWS, :].bitcast(I32).rearrange("r (a c) -> r a c", a=PASSES),
                     scales[:, ROWS * q : ROWS * (q + 1), :].rearrange("a r c -> r a c").bitcast(I32))
 
-        def load_planes_stacked(tile, scales):
-            for q in range(QUADRANTS):
-                nc.sync.dma_start(
+        def load_planes_stacked(tile, scales, queue, quadrants):
+            for q in quadrants:
+                queue.dma_start(
                     tile[QUADRANT * q : QUADRANT * q + PASSES * ROWS, :].bitcast(I32),
                     scales[:, ROWS * q : ROWS * (q + 1), :].bitcast(I32))
 
@@ -109,12 +109,15 @@ def tile_list_photon_triple_coincidence_kernel(
         nc.sync.dma_start(offsets[:], offs)
         load_words(w3_raw[0][:], w3_words[0].rearrange("p c i -> p (c i)"))
         load_planes_apart(tab_s, tab_scales)
+        load_planes_stacked(w3_s_raw, w3_scales, nc.gpsimd, (0,))
+        load_planes_stacked(w3_s_raw, w3_scales, nc.sync, (1,))
         load_table(0)
-        load_planes_stacked(w3_s_raw, w3_scales)
+        load_planes_stacked(w3_s_raw, w3_scales, nc.sync, (2, 3))
         load_table(1)
+        load_planes_side_by_side(w2_s_raw, w2_scales, nc.sync, (3,))
         load_words(w3_raw[1][:], w3_words[1].rearrange("p c i -> p (c i)"))
         load_words(w2_raw[:].rearrange("p (a c) -> p a c", a=PASSES), w2_words.rearrange("a p c -> p a c"))
-        load_planes_side_by_side(w2_s_raw, w2_scales, nc.gpsimd)
+        load_planes_side_by_side(w2_s_raw, w2_scales, nc.gpsimd, (0, 1, 2))
         nc.vector.tensor_copy(v_s0[:], tab_s[:].indirect(offsets[:]))
         nc.sync.dma_start(v_s1[0:SHIFTED, :].bitcast(I32), v_s0[APART:P, :].bitcast(I32))
         load_w1_piece(0)

from contextlib import ExitStack

import concourse.mybir as mybir

K, T, S, H, N = 1024, 2048, 1024, 512, 384
FLOPS = 2 * S * (3 * K * H + H * N + K * N)

F32 = mybir.dt.float32
BF16 = mybir.dt.bfloat16
I32 = mybir.dt.int32
U32 = mybir.dt.uint32
U16 = mybir.dt.uint16
U8 = mybir.dt.uint8
FP8X4 = mybir.dt.float8_e4m3fn_x4
FP4X4 = mybir.dt.float4_e2m1fn_x4
MULT = mybir.AluOpType.mult
ADD = mybir.AluOpType.add

P = 128
PACK = 4
K_PASS = P * PACK
PASSES = K // K_PASS
QUADRANTS, QUADRANT = 4, 32
ROWS = 4
HALF = 512
CHUNK = 256
NT = N // P
PIECE = H // 2
LINE = 16
APART = 16
SHIFTED = P - APART
GATE_PIECE = 256
BANKS = 8
WARM_UPS = 2
ALIGN = 256


def tile_list_photon_triple_coincidence_kernel(
    tc, tab_words, tab_scales, offs, w1, w2_words, w2_scales, w3_words, w3_scales,
    w4, w5_words, w5_scales, eff, out_0, out_1, out_2, out_3,
):
    nc = tc.nc
    with ExitStack() as ctx:
        keep = ctx.enter_context(tc.tile_pool(name="keep", bufs=1))
        placed = ctx.enter_context(tc.tile_pool(name="placed", bufs=1))
        psum = ctx.enter_context(tc.psum_pool(name="psum", bufs=1))

        def held(name, shape, dtype):
            return keep.tile(shape, dtype, name=name, align_bytes=ALIGN)

        def shared(name, tag, shape, dtype):
            return keep.tile(shape, dtype, name=name, tag=tag, align_bytes=ALIGN)

        banks_used = []

        def take_bank(bank, shape):
            banks_used.append(bank)
            return psum.tile(shape, F32, name="sum%d" % len(banks_used), tag="bank%d" % bank)

        offsets = keep.tile([P, S // 16], U16, name="offsets")
        tab_s = held("tab_s", [P, T], U8)
        tab_w = [held("tab_w%d" % a, [P, T], U32) for a in range(PASSES)]
        w3_s_raw = shared("w3_s_raw", "picked01", [P, H], U8)
        w2_s_raw = placed.tile([P, PASSES * H], U8, name="w2_s_raw", offset=0, align_bytes=ALIGN)
        w5_s = held("w5_s", [P, PASSES * N], U8)
        v_s0 = held("v_s0", [P, S], U8)
        v_s1 = held("v_s1", [P, S], U8)
        w3_raw = [shared("w3_raw%d" % a, "w3_raw%d" % a, [P, H], U32) for a in range(PASSES)]
        w2_raw = placed.tile([P, PASSES * H * 2], U8, name="w2_raw", offset=PASSES * H, align_bytes=ALIGN)
        w5_w = held("w5_w", [P, PASSES * N * 2], U8)

        for plane in (tab_s, w3_s_raw, w2_s_raw, v_s1, w5_s):
            nc.vector.memset(plane[:].bitcast(I32), 0)

        def load_planes_side_by_side(tile, scales, queue, quadrants=range(QUADRANTS)):
            for q in quadrants:
                queue.dma_start(
                    tile[QUADRANT * q : QUADRANT * q + ROWS, :].bitcast(I32).rearrange("r (a c) -> r a c", a=PASSES),
                    scales[:, ROWS * q : ROWS * (q + 1), :].rearrange("a r c -> r a c").bitcast(I32))

        def load_planes_stacked(tile, scales, queue, quadrants):
            for q in quadrants:
                queue.dma_start(
                    tile[QUADRANT * q : QUADRANT * q + PASSES * ROWS, :].bitcast(I32),
                    scales[:, ROWS * q : ROWS * (q + 1), :].bitcast(I32))

        def load_planes_apart(tile, scales):
            for r in range(ROWS):
                nc.sync.dma_start(
                    tile[r:P:APART, :].bitcast(I32),
                    scales[:, r : QUADRANTS * ROWS : ROWS, :].rearrange("a q c -> q a c").bitcast(I32))

        def load_words(view, words):
            nc.sync.dma_start(view.bitcast(I32), words.bitcast(I32))

        def load_table(a):
            nc.sync.dma_start(tab_w[a][:].bitcast(I32), tab_words[a].rearrange("p t i -> p (t i)").bitcast(I32))

        w1_raw = {}

        def load_w1_piece(b):
            rows = w1[0:K_PASS, :].rearrange("(p j) c -> p j c", j=PACK)
            w1_raw[0, b] = shared("w1_raw0%d" % b, "piece%d" % b, [P, PACK, PIECE], F32)
            nc.sync.dma_start(w1_raw[0, b][:], rows[:, :, b * PIECE : (b + 1) * PIECE])

        eff_sb = [held("eff%d" % i, [P, S], F32) for i in range(NT)]
        w4_raw = shared("w4_raw", "w4_raw", [P, PACK, N], F32)

        nc.sync.dma_start(offsets[:], offs)
        load_words(w3_raw[0][:], w3_words[0].rearrange("p c i -> p (c i)"))
        load_planes_apart(tab_s, tab_scales)
        load_planes_stacked(w3_s_raw, w3_scales, nc.gpsimd, (0,))
        load_planes_stacked(w3_s_raw, w3_scales, nc.sync, (1,))
        load_table(0)
        load_planes_stacked(w3_s_raw, w3_scales, nc.sync, (2, 3))
        load_table(1)
        load_planes_side_by_side(w2_s_raw, w2_scales, nc.sync, (3,))
        load_words(w3_raw[1][:], w3_words[1].rearrange("p c i -> p (c i)"))
        load_words(w2_raw[:].rearrange("p (a c) -> p a c", a=PASSES), w2_words.rearrange("a p c -> p a c"))
        load_planes_side_by_side(w2_s_raw, w2_scales, nc.gpsimd, (0, 1, 2))
        nc.vector.tensor_copy(v_s0[:], tab_s[:].indirect(offsets[:]))
        nc.sync.dma_start(v_s1[0:SHIFTED, :].bitcast(I32), v_s0[APART:P, :].bitcast(I32))
        load_w1_piece(0)
        load_w1_piece(1)
        w1_pass1 = shared("w1_raw1", "pass1", [P, PACK, H], F32)
        nc.sync.dma_start(w1_pass1[:], w1[K_PASS:K, :].rearrange("(p j) c -> p j c", j=PACK))
        for b in range(2):
            w1_raw[1, b] = w1_pass1[:, :, b * PIECE : (b + 1) * PIECE]
        load_words(w5_w[:].rearrange("p (a c) -> p a c", a=PASSES), w5_words.rearrange("a p c -> p a c"))
        load_planes_side_by_side(w5_s, w5_scales, nc.gpsimd)
        nc.sync.dma_start(w4_raw[:], w4.rearrange("(p j) n -> p j n", j=PACK))
        for i in range(NT):
            nc.sync.dma_start(eff_sb[i][:], eff[i * P : (i + 1) * P, :])

        v_s = [v_s0, v_s1]
        v_w = {}
        w3_w = [held("w3_w%d" % a, [P, PACK * P], U32) for a in range(PASSES)]
        w3_s = held("w3_s", [P, PACK * P], U8)
        w2_w = held("w2_w", [P, PACK * PASSES * P * 2], U8)

        def deal_lines(dst, src, size):
            run = LINE // size
            nc.vector.tensor_copy(
                dst.rearrange("p (t g i) -> p g t i", t=PACK, i=run),
                src.rearrange("p (g i t) -> p g t i", t=PACK, i=run))

        def deal_in_order(dst, src):
            nc.scalar.copy(dst.rearrange("p (t m) -> p m t", t=PACK), src.rearrange("p (m t) -> p m t", t=PACK))

        def gather_words(a, hf, tag):
            if tag:
                v_w[a, hf] = shared("v_w%d%d" % (a, hf), tag, [P, HALF], U32)
            else:
                v_w[a, hf] = placed.tile([P, HALF], U32, name="v_w11", offset=0, align_bytes=ALIGN)
            entries = offsets[:, hf * HALF // 16 : (hf + 1) * HALF // 16]
            nc.vector.tensor_copy(v_w[a, hf][:], tab_w[a][:].indirect(entries))

        deal_in_order(w3_w[0][:], w3_raw[0][:])
        deal_in_order(w3_w[1][:], w3_raw[1][:])
        deal_in_order(w2_w[:].bitcast(U16), w2_raw[:].bitcast(U16))
        gather_words(0, 0, "picked00")
        deal_lines(w3_s[:], w3_s_raw[:], 1)
        gather_words(0, 1, "picked01")
        gather_words(1, 0, "picked10")
        w2_s = shared("w2_s", "w3_raw1", [P, PACK * PASSES * P], U8)
        deal_lines(w2_s[:], w2_s_raw[:], 1)
        gather_words(1, 1, None)

        def dealt_cols(t, a, width):
            return slice((t * PASSES + a) * width, (t * PASSES + a + 1) * width)

        w1_b = [held("w1_b%d" % a, [P, PACK * H], BF16) for a in range(PASSES)]
        w1_w = [held("w1_w%d" % a, [P, H], U32) for a in range(PASSES)]
        w1_s = [held("w1_s%d" % a, [P, H], U8) for a in range(PASSES)]

        def round_w1(a, b, round_copy, walk):
            places = slice(b * PIECE // PACK, (b + 1) * PIECE // PACK)
            round_copy(
                w1_b[a][:].rearrange("p (t m j) -> p m " + walk, t=PACK, j=PACK)[:, places],
                w1_raw[a, b][:].rearrange("p j (m t) -> p m " + walk, t=PACK))

        def quantize_w1(a):
            nc.vector.quantize_mx(out=w1_w[a][:].bitcast(FP8X4), scales=w1_s[a][:], in_=w1_b[a][:])

        d3_banks, d3, d23 = {}, {}, {}

        def w3_pass(hf, a, slices, first_bank=None):
            for t in slices:
                if a == 0:
                    d3_banks[t, hf] = take_bank(first_bank + t - slices[0], [P, HALF])
                nc.tensor.matmul_mx(
                    out=d3_banks[t, hf][:], lhsT=w3_w[a][:, t * P : (t + 1) * P].bitcast(FP8X4),
                    lhsT_scale=w3_s[ROWS * a : P, t * P : (t + 1) * P],
                    rhs=v_w[a, hf][:].bitcast(FP8X4), rhs_scale=v_s[a][:, hf * HALF : (hf + 1) * HALF],
                    start=(a == 0), stop=(a == PASSES - 1))

        def hold_d3(name, tag, sums):
            whole = shared(name, tag, [P, len(sums), HALF], F32)
            for place, (t, hf) in enumerate(sums):
                d3[hf, t] = whole[:, place, :]

        def copy_d3(t, hf):
            nc.scalar.copy(d3[hf, t], d3_banks[t, hf][:])

        def make_d23(t, hf, number):
            bank = take_bank(number, [P, HALF])
            for a in range(PASSES):
                nc.tensor.matmul_mx(
                    out=bank[:], lhsT=w2_w[:, dealt_cols(t, a, 2 * P)].bitcast(FP4X4),
                    lhsT_scale=w2_s[:, dealt_cols(t, a, P)],
                    rhs=v_w[a, hf][:].bitcast(FP8X4), rhs_scale=v_s[a][:, hf * HALF : (hf + 1) * HALF],
                    start=(a == 0), stop=(a == PASSES - 1))
            if t % 2 == 0:
                name = "d23_%d%d" % (hf, t // 2)
                d23[hf, t // 2] = shared(name, name if t + hf else "piece0", [P, 2, HALF], F32)
            nc.vector.tensor_tensor(d23[hf, t // 2][:, t % 2, :], bank[:], d3[hf, t], MULT)

        w4_b = shared("w4_b", "w4_b", [P, N * PACK], BF16)
        w4_w = {}
        w4_s = held("w4_s", [P, N], U8)

        def round_w4():
            nc.scalar.copy(
                w4_b[:].rearrange("p (c i j) -> p c j i", i=LINE // 4, j=PACK),
                w4_raw[:].rearrange("p j (c i) -> p c j i", i=LINE // 4))

        def quantize_w4():
            w4_w[0] = shared("w4_w", "pass1", [P, N], U32)
            nc.vector.quantize_mx(out=w4_w[0][:].bitcast(FP8X4), scales=w4_s[:], in_=w4_b[:])

        h_w = {}
        h_s = held("h_s", [P, S], U8)
        lin = {}
        gated = {}
        h_b = [shared("h_b%d" % hf, "h_b%d" % hf, [P, HALF * PACK], BF16) for hf in range(2)]
        h = [held("h%d" % hf, [P, PACK, HALF], F32) for hf in range(2)]
        y = [held("y%d" % hf, [P, NT, HALF], F32) for hf in range(2)]

        def chunk(c):
            hf, lo = divmod(c * CHUNK, HALF)
            return hf, slice(lo, lo + CHUNK), slice(c * CHUNK, (c + 1) * CHUNK)

        def w5_product(hf, i, number):
            bank = take_bank(number, [P, HALF])
            for a in range(PASSES):
                first = a * N + i * P
                nc.tensor.matmul_mx(
                    out=bank[:], lhsT=w5_w[:, 2 * first : 2 * (first + P)].bitcast(FP4X4),
                    lhsT_scale=w5_s[:, first : first + P],
                    rhs=v_w[a, hf][:].bitcast(FP8X4), rhs_scale=v_s[a][:, hf * HALF : (hf + 1) * HALF],
                    start=(a == 0), stop=(a == PASSES - 1))
            return bank

        def w5_sum(hf, i, number):
            bank = w5_product(hf, i, number)
            if i == 0:
                lin[hf] = shared("lin%d" % hf, "lin1" if hf else "w4_raw", [P, NT, HALF], F32)
            nc.scalar.copy(lin[hf][:, i, :], bank[:])

        def gate_on_vector(hf, i, number):
            bank = w5_product(hf, i, number)
            nc.vector.tensor_tensor(gated[hf, i], bank[:], eff_sb[i][:, hf * HALF : (hf + 1) * HALF], MULT)

        def hold_gated(name, tag, sums):
            whole = shared(name, tag, [P, len(sums), HALF], F32)
            for place, key in enumerate(sums):
                gated[key] = whole[:, place, :]

        def gate(hf, i, piece=HALF):
            for lo in range(0, HALF, piece):
                nc.gpsimd.tensor_tensor(
                    gated[hf, i][:, lo : lo + piece], lin[hf][:, i, lo : lo + piece],
                    eff_sb[i][:, hf * HALF + lo : hf * HALF + lo + piece], MULT)

        def make_h_pair(c, pair, number):
            hf, in_half, in_list = chunk(c)
            bank = take_bank(number, [P, 2, CHUNK])
            for e in range(2):
                t = 2 * pair + e
                for a in range(PASSES):
                    nc.tensor.matmul_mx(
                        out=bank[:, e, :], lhsT=w1_w[a][:, t * P : (t + 1) * P].bitcast(FP8X4),
                        lhsT_scale=w1_s[a][:, t * P : (t + 1) * P],
                        rhs=v_w[a, hf][:, in_half].bitcast(FP8X4), rhs_scale=v_s[a][:, in_list],
                        start=(a == 0), stop=(a == PASSES - 1))
            nc.vector.tensor_tensor(
                h[hf][:, 2 * pair : 2 * pair + 2, in_half], bank[:], d23[hf, pair][:, :, in_half], MULT)
            if pair == 1:
                nc.sync.dma_start(out_1[:, in_list].rearrange("(p t) j -> p t j", t=PACK), h[hf][:, :, in_half])

        def make_h(c, numbers):
            for pair in range(PACK // 2):
                make_h_pair(c, pair, numbers[pair])

        def round_h(c):
            hf, in_half = chunk(c)[:2]
            nc.scalar.copy(
                h_b[hf][:, PACK * in_half.start : PACK * in_half.stop].rearrange("p (c i t) -> p c t i", i=LINE // 4, t=PACK),
                h[hf][:, :, in_half].rearrange("p t (c i) -> p c t i", i=LINE // 4))

        def quantize_h(hf):
            cols = slice(hf * HALF, (hf + 1) * HALF)
            h_w[hf] = shared("h_w%d" % hf, "w4_b" if hf else "h_w0", [P, HALF], U32)
            nc.vector.quantize_mx(out=h_w[hf][:].bitcast(FP8X4), scales=h_s[:, cols], in_=h_b[hf][:])
            nc.sync.dma_start(
                out_2[0, :, cols, :].rearrange("p m t -> p (m t)").bitcast(I32), h_w[hf][:].bitcast(I32))
            if cols.stop == S:
                for q in range(QUADRANTS):
                    nc.scalar.dma_start(
                        out_3[0, ROWS * q : ROWS * (q + 1), :].bitcast(I32),
                        h_s[QUADRANT * q : QUADRANT * q + ROWS, :].bitcast(I32))

        def make_y(hf, i, number):
            cols = slice(hf * HALF, (hf + 1) * HALF)
            bank = take_bank(number, [P, HALF])
            nc.tensor.matmul_mx(
                out=bank[:], lhsT=w4_w[0][:, i * P : (i + 1) * P].bitcast(FP8X4), lhsT_scale=w4_s[:, i * P : (i + 1) * P],
                rhs=h_w[hf][:].bitcast(FP8X4), rhs_scale=h_s[:, cols], start=True, stop=True)
            nc.vector.tensor_tensor(y[hf][:, i, :], bank[:], gated[hf, i], ADD)
            nc.sync.dma_start(out_0[i * P : (i + 1) * P, cols], y[hf][:, i, :])

        warm = take_bank(BANKS - 1, [P, HALF])
        for unused in range(WARM_UPS):
            nc.tensor.matmul_mx(
                out=warm[:], lhsT=w3_raw[0][:, 0:P].bitcast(FP8X4), lhsT_scale=w3_s_raw[:, 0:P],
                rhs=w3_raw[0][:].bitcast(FP8X4), rhs_scale=w3_s_raw[:], start=True, stop=True)
        w3_pass(0, 0, (0, 1, 2, 3), 0)
        w3_pass(1, 0, (0, 1, 2), 4)
        w3_pass(0, 1, (0, 1, 2, 3))
        round_w1(0, 0, nc.vector.tensor_copy, "j t")
        hold_d3("d3_a", "d3_a", ((0, 0), (1, 0), (2, 0), (3, 0)))
        for t, number in ((0, 7), (1, 0)):
            copy_d3(t, 0)
            make_d23(t, 0, number)
        w3_pass(1, 1, (0, 1, 2))
        for t in (2, 3):
            copy_d3(t, 0)
            make_d23(t, 0, t - 1)
        round_w1(0, 1, nc.scalar.copy, "j t")
        quantize_w1(0)
        hold_d3("d3_b", "piece1", ((0, 1), (1, 1)))
        copy_d3(0, 1)
        make_d23(0, 1, 7)
        w3_pass(1, 0, (3,), 3)
        w3_pass(1, 1, (3,))
        round_w1(1, 1, nc.vector.tensor_copy, "j t")
        copy_d3(1, 1)
        make_d23(1, 1, 0)
        round_w1(1, 0, nc.scalar.copy, "j t")
        quantize_w1(1)
        hold_d3("d3_c", "pass1", ((2, 1), (3, 1)))
        for t in (2, 3):
            copy_d3(t, 1)
            make_d23(t, 1, t - 1)
        round_w4()
        w5_sum(0, 0, 7)
        w5_sum(0, 1, 4)
        make_h(0, (5, 0))
        make_h_pair(1, 0, 6)
        quantize_w4()
        hold_gated("gated_a", "w4_b", ((0, 0), (0, 1)))
        gate(0, 0)
        gate(0, 1)
        make_h_pair(1, 1, 3)
        round_h(0)
        hold_gated("gated_b", "gated_b", ((0, 2),))
        make_h(2, (2, 5))
        w5_sum(0, 2, 6)
        gate(0, 2, GATE_PIECE)
        round_h(1)
        make_h(3, (1, 0))
        w5_sum(1, 0, 2)
        quantize_h(0)
        round_h(2)
        hold_gated("gated_c", "h_b0", ((1, 0), (1, 2)))
        gate(1, 0)
        gate_on_vector(1, 2, 5)
        make_y(0, 0, 4)
        round_h(3)
        w5_sum(1, 1, 0)
        make_y(0, 1, 7)
        quantize_h(1)
        hold_gated("gated_d", "h_b1", ((1, 1),))
        gate(1, 1)
        make_y(0, 2, 3)
        make_y(1, 0, 6)
        make_y(1, 2, 1)
        make_y(1, 1, 2)
